import numpy as np
import ml_dtypes


def mxq(x, axis, fmt="e4m3"):
    dtype, down = {"e4m3": (ml_dtypes.float8_e4m3fn, 7), "e5m2": (ml_dtypes.float8_e5m2, 14)}[fmt]
    v = np.moveaxis(np.asarray(x, np.float32).astype(ml_dtypes.bfloat16).astype(np.float64), axis, -1)
    blocks = v.reshape(v.shape[:-1] + (-1, 32))
    amax = np.abs(blocks).max(-1, keepdims=True)
    byte = np.maximum(np.where(amax > 0, np.frexp(amax)[1] - 1 + 127, 0) - down, 1)
    scale = np.exp2(byte - 127.0)
    codes = (blocks / scale).astype(np.float32).astype(dtype).astype(np.float64)
    return np.moveaxis((codes * scale).reshape(v.shape), -1, axis)


WIDE = False


def mx_kscale(k):
    if not WIDE:
        return np.ones(k)
    levels = np.array([10, -10, 5, -5, 0])
    if k % 512:
        return np.exp2(np.random.permutation(np.resize(levels, k // 32))).repeat(32)
    a = np.empty((k // 512, 16))
    for p in range(k // 512):
        a[p, :8] = np.random.permutation(np.resize(levels, 8))
        for g in range(8):
            far = levels[np.abs(levels - a[p, g]) >= 10]
            a[p, g + 8] = far[np.random.randint(len(far))]
    return np.exp2(a.ravel()).repeat(32)


def f64(x):
    return np.asarray(x).astype(np.float64)


def striped(idx):
    return np.tile(idx.reshape(-1, 16).T, (8, 1)).astype(np.uint16)


def unstriped(offs):
    return offs[:16].T.reshape(-1).astype(np.int64)


E2M1 = np.array([0.0, 0.5, 1.0, 1.5, 2.0, 3.0, 4.0, 6.0, -0.0, -0.5, -1.0, -1.5, -2.0, -3.0, -4.0, -6.0])


def pack_weight(w, fmt):
    k, n = w.shape
    w = f64(np.asarray(w, np.float32).astype(ml_dtypes.bfloat16)).reshape(k // 32, 32, n)
    amax = np.abs(w).max(1)
    if fmt == "e4m3":
        byte = np.frexp(amax)[1] - 1 + 127 - 7
    else:
        mant, ex = np.frexp(amax / 6.0)
        byte = np.where(mant > 0.5, ex, ex - 1) + 127
    byte = np.clip(np.where(amax > 0, byte, 1), 1, 254)
    scaled = (w * np.exp2(127.0 - byte)[:, None, :]).reshape(k, n).astype(np.float32)
    by_word = np.ascontiguousarray(scaled.reshape(k // 512, 128, 4, n).transpose(0, 1, 3, 2))
    if fmt == "e4m3":
        words = by_word.astype(ml_dtypes.float8_e4m3fn).view(np.uint8)
    else:
        c = by_word.astype(ml_dtypes.float4_e2m1fn).view(np.uint8) & 0xF
        words = (c[..., 0::2] | (c[..., 1::2] << 4)).reshape(k // 512, 128, 2 * n)
    return np.ascontiguousarray(words), np.ascontiguousarray(byte.astype(np.uint8).reshape(k // 512, 16, n))


def unpack_weight(words, scales, fmt):
    g, _, n = scales.shape
    words = np.ascontiguousarray(words).reshape(g, 128, n, -1)
    if fmt == "e4m3":
        vals = words.view(ml_dtypes.float8_e4m3fn).astype(np.float64)
    else:
        nib = np.empty((g, 128, n, 4), np.uint8)
        nib[..., 0::2] = words & 0xF
        nib[..., 1::2] = words >> 4
        vals = E2M1[nib]
    vals = vals * np.repeat(np.exp2(scales.astype(np.float64) - 127.0), 8, axis=1)[..., None]
    return vals.transpose(0, 1, 3, 2).reshape(g * 512, n)


def gelu(v):
    return 0.5 * v * (1.0 + np.tanh(np.sqrt(2.0 / np.pi) * (v + 0.044715 * v**3)))


K, H, N, T, S, T2, P = 1024, 1024, 384, 4096, 1024, 2048, 1024

def setup_inputs():
    n = np.random.standard_normal
    s = mx_kscale(K)[:, None]
    u = mx_kscale(H)[:, None]
    d = {}
    d["tab_words"], d["tab_scales"] = pack_weight(n((K, T)) * s, "e4m3")
    d["offs"] = striped(np.random.permutation(T)[:S])
    d["offs2"] = striped(np.random.permutation(T2)[:S])
    d["offs3"] = striped(np.random.permutation(T2)[:P])
    d["offs4"] = striped(np.random.permutation(T2)[:P])
    d["w1"] = (2.5 * n((K, H)) / K**0.5 / s).astype(np.float32)
    d["usual"] = (0.8 + 0.6 * n((H, S))).astype(np.float32)
    d["gain"] = (np.exp(0.3 * n(H)) * u[:, 0]).astype(np.float32)
    d["wgs"] = np.exp(0.3 * n((128, S))).astype(np.float32)
    d["page0"] = (n((H, T2)) * u).astype(np.float32)
    d["low"] = (0.5 * n(H) * u[:, 0]).astype(np.float32)
    d["wr_words"], d["wr_scales"] = pack_weight(1.5 * n((H, N)) / H**0.5 / u, "e2m1")
    d["wn"] = (1.5 * n((K, N)) / K**0.5 / s).astype(np.float32)
    d["wh_words"], d["wh_scales"] = pack_weight(1.2 * n((H, N)) / H**0.5 / u, "e4m3")
    d["wgo"] = np.exp(0.3 * n((128, P))).astype(np.float32)
    d["page1"] = n((N, T2)).astype(np.float32)
    return d

def reference(tab_words, tab_scales, offs, offs2, offs3, offs4, w1, usual, gain, wgs, page0, low, wr_words, wr_scales, wn, wh_words, wh_scales, wgo, page1):
    v = unpack_weight(tab_words, tab_scales, "e4m3")[:, unstriped(offs)]
    a = mxq(f64(w1), 0, "e4m3").T @ v
    h = (np.log(1.0 + np.abs(a)) - f64(usual)) * f64(gain)[:, None]
    page = f64(page0).copy()
    page[:, unstriped(offs2)] = np.tile(f64(wgs), (H // 128, 1)) * h
    x = np.maximum(page[:, unstriped(offs3)], f64(low)[:, None])
    recalled = unpack_weight(wr_words, wr_scales, "e2m1").T @ mxq(x, 0, "e4m3")
    notes = mxq(f64(wn), 0, "e4m3").T @ v
    state = unpack_weight(wh_words, wh_scales, "e4m3").T @ mxq(h, 0, "e4m3")
    y = np.maximum(recalled, notes) - state
    out = f64(page1).copy()
    out[:, unstriped(offs4)] = np.tile(f64(wgo), (N // 128, 1)) * y
    return out

@@ -1,0 +1,438 @@
+from contextlib import ExitStack
+
+import concourse.mybir as mybir
+from concourse.masks import make_identity
+
+K, H, N, T, S, T2 = 1024, 1024, 384, 4096, 1024, 2048
+FLOPS = 2 * K * H * S + 3 * 2 * K * N * S
+
+F32 = mybir.dt.float32
+BF16 = mybir.dt.bfloat16
+I32 = mybir.dt.int32
+U32 = mybir.dt.uint32
+U16 = mybir.dt.uint16
+U8 = mybir.dt.uint8
+FP8X4 = mybir.dt.float8_e4m3fn_x4
+FP4X4 = mybir.dt.float4_e2m1fn_x4
+ALU = mybir.AluOpType
+ACT = mybir.ActivationFunctionType
+
+P = 128
+PACK = 4
+PASS = P * PACK
+PASSES = 2
+HALF = 512
+BLOCKS = HALF // P
+OUT_TILES = N // P
+LIST_COLS = S // 16
+
+
+def tile_list_visit_page_update_kernel(
+    tc, tab_words, tab_scales, offs, offs2, offs3, offs4, w1, usual, gain, wgs, page0, low,
+    wr_words, wr_scales, wn, wh_words, wh_scales, wgo, page1, out,
+):
+    nc = tc.nc
+    with ExitStack() as ctx:
+        lists = ctx.enter_context(tc.tile_pool(name="lists", bufs=1))
+        keep = ctx.enter_context(tc.tile_pool(name="keep", bufs=1))
+        ring = ctx.enter_context(tc.tile_pool(name="ring", bufs=2))
+        psum = ctx.enter_context(tc.psum_pool(name="psum", bufs=2))
+
+        def kept(shape, dtype, name):
+            return keep.tile(shape, dtype, name=name, align_bytes=64)
+
+        def half_cols(hf):
+            return slice(hf * HALF, (hf + 1) * HALF)
+
+        def half_list(tile, hf):
+            return tile[:, hf * LIST_COLS // 2 : (hf + 1) * LIST_COLS // 2]
+
+        def load_list(src, name):
+            tile = lists.tile([P, LIST_COLS], U16, name=name)
+            nc.sync.dma_start(tile[:], src)
+            return tile
+
+        def slice_rows(src, s):
+            b, t = divmod(s, PACK)
+            return src.rearrange("(b p t) c -> b t p c", b=PASSES, t=PACK)[b, t]
+
+        def load_weight_rows(src, a, cols, name):
+            width = cols.stop - cols.start
+            raw = ring.tile([P, PACK, width], F32, name=name, tag="raw8k", bufs=3)
+            nc.sync.dma_start(raw[:], src[a * PASS : (a + 1) * PASS, cols].rearrange("(p j) c -> p j c", j=PACK))
+            return raw
+
+        usual_buf = [kept([P, S], F32, "usual_buf%d" % i) for i in range(4)]
+
+        def load_usual(s):
+            nc.sync.dma_start(usual_buf[s % 4][:], slice_rows(usual, s))
+
+        def load_page(s):
+            if s == 7:
+                tile = ring.tile([P, T2], F32, name="page7", tag="last_page", bufs=1)
+            else:
+                tile = ring.tile([P, T2], F32, name="page%d" % s, tag="page", bufs=4)
+            nc.sync.dma_start(tile[:], slice_rows(page0, s))
+            return tile
+
+        def load_table(a):
+            tile = ring.tile([P, T], U32, name="table%d" % a, tag="big%d" % a, bufs=1)
+            nc.sync.dma_start(tile[:].bitcast(I32), tab_words[a].rearrange("p n t -> p (n t)").bitcast(I32))
+            return tile
+
+        def load_weight_scales(src, name):
+            tile = kept([P, PASSES, N], U8, name)
+            nc.vector.memset(tile[:].rearrange("p a n -> p (a n)").bitcast(I32), 0)
+            return tile
+
+        def fill_weight_scales(tile, src):
+            for q in range(4):
+                nc.sync.dma_start(
+                    tile[32 * q : 32 * q + 4, :, :].bitcast(I32),
+                    src[:, 4 * q : 4 * q + 4, :].rearrange("a r n -> r a n").bitcast(I32),
+                )
+
+        table_scales = ring.tile([P, T], U8, name="table_scales", tag="early_late", bufs=1)
+        nc.vector.memset(table_scales[:].bitcast(I32), 0)
+        warm = kept([P, 8], F32, "warm")
+        nc.vector.memset(warm[:], 1.0)
+        nc.scalar.activation(warm[:], warm[:], ACT.Ln)
+        wr_sc = load_weight_scales(wr_scales, "wr_sc")
+        wh_sc = load_weight_scales(wh_scales, "wh_sc")
+        ident = kept([P, P], F32, "ident")
+        make_identity(nc, ident[:])
+
+        w1_raw = {}
+        scale_rows = ring.tile([P, T], U8, name="scale_rows", tag="staging", bufs=3, align_bytes=64)
+        for q in range(4):
+            nc.sync.dma_start(
+                scale_rows[32 * q : 32 * q + 8, :].bitcast(I32),
+                tab_scales[:, 4 * q : 4 * q + 4, :].bitcast(I32),
+            )
+        w1_raw[0, 0] = load_weight_rows(w1, 0, half_cols(0), "w1_raw00")
+        table = [load_table(0)]
+        idx = load_list(offs, "idx")
+        w1_raw[1, 0] = load_weight_rows(w1, 1, half_cols(0), "w1_raw10")
+        table.append(load_table(1))
+        gain_t = kept([P, PASSES, PACK], F32, "gain_t")
+        nc.sync.dma_start(gain_t[:], gain.rearrange("(b p t) -> p b t", b=PASSES, t=PACK))
+        idx2 = load_list(offs2, "idx2")
+        load_usual(0)
+        page = [load_page(0)]
+        wgs_rows = wgs.rearrange("(i t) j -> i t j", t=PACK)
+        wgs_first = kept([P, S], F32, "wgs_first")
+        for q in range(4):
+            nc.sync.dma_start(wgs_first[32 * q : 32 * q + 32, :], wgs_rows[:, 0, :])
+        load_usual(1)
+        idx3 = load_list(offs3, "idx3")
+        low_t = kept([P, PASSES, PACK], F32, "low_t")
+        nc.sync.dma_start(low_t[:], low.rearrange("(b p t) -> p b t", b=PASSES, t=PACK))
+        wgs_rest = kept([P, PACK - 1, S], F32, "wgs_rest")
+        for q in range(4):
+            nc.sync.dma_start(wgs_rest[32 * q : 32 * q + 32, :, :], wgs_rows[:, 1:PACK, :])
+        page.append(load_page(1))
+        w1_raw[0, 1] = load_weight_rows(w1, 0, half_cols(1), "w1_raw01")
+        w1_raw[1, 1] = load_weight_rows(w1, 1, half_cols(1), "w1_raw11")
+        load_usual(2)
+        page.append(load_page(2))
+        wn_raw = [load_weight_rows(wn, a, slice(0, N), "wn_raw%d" % a) for a in range(PASSES)]
+        load_usual(3)
+        page.append(load_page(3))
+        wr_t = kept([P, PASSES, 2 * N], U8, "wr_t")
+        wh_t = kept([P, PASSES, N], U32, "wh_t")
+        late = {}
+        visit = []
+
+        def last_loads():
+            fill_weight_scales(wr_sc, wr_scales)
+            fill_weight_scales(wh_sc, wh_scales)
+            nc.sync.dma_start(wr_t[:].bitcast(I32), wr_words.rearrange("a p c -> p a c").bitcast(I32))
+            nc.sync.dma_start(wh_t[:].bitcast(I32), wh_words.rearrange("a p n t -> p a (n t)").bitcast(I32))
+            late["idx4"] = load_list(offs4, "idx4")
+            late["wgo"] = ring.tile([P, S], F32, name="wgo_t", tag="early_late", bufs=1)
+            nc.sync.dma_start(late["wgo"][:], wgo)
+            for nb in range(OUT_TILES):
+                tile = ring.tile([P, T2], F32, name="visit%d" % nb, tag="raw8k", bufs=3)
+                nc.sync.dma_start(tile[:], page1[nb * P : (nb + 1) * P, :])
+                visit.append(tile)
+
+        def wgs_slice(t):
+            return wgs_first[:] if t == 0 else wgs_rest[:, t - 1, :]
+
+        def staging(name):
+            return ring.tile([P, PACK * HALF], BF16, name=name, tag="staging", bufs=3, align_bytes=64)
+
+        def mx_operand(width, name):
+            return kept([P, width], U32, name + "_codes"), kept([P, width], U8, name + "_scales")
+
+        def quantize(operand, cols, src):
+            codes, scales = operand
+            nc.vector.quantize_mx(out=codes[:, cols].bitcast(FP8X4), scales=scales[:, cols], in_=src)
+
+        def cast_w1(a, b, copy):
+            stage = staging("w1_bf%d%d" % (a, b))
+            copy(
+                stage[:].rearrange("p (t m j) -> p m j t", t=PACK, j=PACK),
+                w1_raw[a, b][:].rearrange("p j (m t) -> p m j t", t=PACK),
+            )
+            return stage
+
+        def interleave(src, stage):
+            width = src.shape[2]
+            nc.scalar.copy(
+                stage[:, 0 : PACK * width].rearrange("p (c i t) -> p c t i", i=4, t=PACK),
+                src.rearrange("p t (c i) -> p c t i", i=4),
+            )
+            return stage
+
+        def work(name):
+            return ring.tile([P, HALF], F32, name=name, tag="work", bufs=5)
+
+        def add_transposed(dst, first, second):
+            nc.tensor.matmul(dst, lhsT=first, rhs=ident[:], is_transpose=True, start=True, stop=False)
+            nc.tensor.matmul(dst, lhsT=second, rhs=ident[:], is_transpose=True, start=False, stop=True)
+
+        w1_q = {}
+        for a in range(PASSES):
+            for b in range(PASSES):
+                w1_q[a, b] = mx_operand(HALF, "w1q%d%d" % (a, b))
+        v_scales = kept([P, S], U8, "v_scales")
+        v_codes = [kept([P, S], U32, "v_codes%d" % a) for a in range(PASSES)]
+        whole = slice(0, HALF)
+        stage = cast_w1(0, 0, nc.vector.tensor_copy)
+        for q in range(4):
+            rows = slice(32 * q, 32 * q + 8)
+            nc.vector.tensor_copy(table_scales[rows, :].bitcast(I32), scale_rows[rows, :].bitcast(I32))
+        nc.vector.tensor_copy(v_scales[:], table_scales[:].indirect(idx[:]))
+        quantize(w1_q[0, 0], whole, stage[:])
+        nc.vector.tensor_copy(v_codes[0][:], table[0][:].indirect(idx[:]))
+        stage = cast_w1(1, 0, nc.vector.tensor_copy)
+        quantize(w1_q[1, 0], whole, stage[:])
+        for hf in range(2):
+            nc.vector.tensor_copy(v_codes[1][:, half_cols(hf)], table[1][:].indirect(half_list(idx, hf)))
+
+        h_t = {}
+        shared = kept([P, 2 * S], F32, "shared")
+
+        def make_h(s, hf):
+            b, t = divmod(s, PACK)
+            if b not in h_t:
+                h_t[b] = ring.tile([P, PACK, S], F32, name="h%d" % b, tag="big%d" % b, bufs=1)
+            usual_bank = psum.tile([P, HALF], F32, name="usual_bank", tag="bank_u", bufs=2)
+            for jb in range(BLOCKS):
+                j0 = hf * HALF + jb * P
+                nc.tensor.transpose(usual_bank[:, jb * P : (jb + 1) * P], usual_buf[s % 4][:, j0 : j0 + P], ident[:])
+            neg_usual = work("neg_usual")
+            nc.scalar.activation(neg_usual[:], usual_bank[:], ACT.Copy, scale=-1.0)
+            a_bank = psum.tile([P, HALF], F32, name="a_bank", tag="bank_a", bufs=2)
+            for jb in range(BLOCKS):
+                j0 = hf * HALF + jb * P
+                for a in range(PASSES):
+                    codes, scales = w1_q[a, b]
+                    nc.tensor.matmul_mx(
+                        out=a_bank[:, jb * P : (jb + 1) * P],
+                        lhsT=v_codes[a][:, j0 : j0 + P].bitcast(FP8X4),
+                        lhsT_scale=v_scales[4 * a : P, j0 : j0 + P],
+                        rhs=codes[:, t * P : (t + 1) * P].bitcast(FP8X4),
+                        rhs_scale=scales[:, t * P : (t + 1) * P],
+                        start=(a == 0),
+                        stop=(a == PASSES - 1),
+                    )
+            if s == 5:
+                logs = shared[:, (1 - hf) * S : (1 - hf) * S + HALF]
+            elif s == 7 and hf == 1:
+                logs = ring.tile([P, HALF], F32, name="logs_last", tag="last_page", bufs=1)[:]
+            else:
+                logs = work("logs")[:]
+            nc.scalar.activation(logs, a_bank[:], ACT.Abs)
+            nc.scalar.activation(logs, logs, ACT.Ln, bias=1.0)
+            h_bank = psum.tile([P, HALF], F32, name="h_bank", tag="bank_h", bufs=4)
+            for jb in range(BLOCKS):
+                cols = slice(jb * P, (jb + 1) * P)
+                add_transposed(h_bank[:, cols], neg_usual[:, cols], logs[:, cols])
+            nc.scalar.activation(h_t[b][:, t, half_cols(hf)], h_bank[:], ACT.Copy, scale=gain_t[:, b, t : t + 1])
+
+        def scatter_h(s, hf):
+            b, t = divmod(s, PACK)
+            if hf is None:
+                nc.vector.tensor_tensor(page[s][:].indirect(idx2[:]), h_t[b][:, t, :], wgs_slice(t), ALU.mult)
+            else:
+                nc.vector.tensor_tensor(
+                    page[s][:].indirect(half_list(idx2, hf)), h_t[b][:, t, half_cols(hf)],
+                    wgs_slice(t)[:, half_cols(hf)], ALU.mult,
+                )
+
+        picked = [kept([P, S], F32, "picked%d" % i) for i in range(2)]
+        x_rows = [kept([P, PACK, S], BF16, "x_rows%d" % b) for b in range(PASSES)]
+
+        def gather_x(s, hf, dst):
+            if hf is None:
+                nc.vector.tensor_copy(dst, page[s][:].indirect(idx3[:]))
+            else:
+                nc.vector.tensor_copy(dst, page[s][:].indirect(half_list(idx3, hf)))
+
+        def floor_x(s, cols, src):
+            b, t = divmod(s, PACK)
+            nc.vector.tensor_scalar(x_rows[b][:, t, cols], src, low_t[:, b, t : t + 1], None, op0=ALU.max)
+
+        h_q = [mx_operand(S, "hq%d" % b) for b in range(PASSES)]
+        x_q = [mx_operand(S, "xq%d" % b) for b in range(PASSES)]
+        wn_q = mx_operand(PASSES * N, "wnq")
+
+        def quantize_rows(operand, rows, cols, stage):
+            interleave(rows[:, :, cols], stage)
+            quantize(operand, cols, stage[:, 0 : PACK * (cols.stop - cols.start)])
+
+        def quantize_wn(a):
+            stage = interleave(wn_raw[a][:], staging("wn_bf%d" % a))
+            quantize(wn_q, slice(a * N, a * N + 256), stage[:, 0:1024])
+            quantize(wn_q, slice(a * N + 256, (a + 1) * N), stage[:, 1024 : PACK * N])
+
+        def first_pick(s):
+            return (None, slice(0, S)) if s < PACK else (0, whole)
+
+        units = [slice(0, 256), slice(256, 512), slice(512, 1024)]
+
+        clock = kept([P, 8], F32, "clock")
+        make_h(0, 0)
+        scatter_h(0, 0)
+        make_h(0, 1)
+        scatter_h(0, 1)
+        load_usual(4)
+        page.append(load_page(4))
+        for hf in range(2):
+            make_h(1, hf)
+        load_usual(5)
+        scatter_h(1, None)
+        gather_x(0, None, picked[0][:])
+        for a in range(PASSES):
+            quantize(w1_q[a, 1], whole, cast_w1(a, 1, nc.scalar.copy)[:])
+        for s in range(2, 8):
+            for hf in range(2):
+                make_h(s, hf)
+            if s == 2:
+                load_usual(6)
+                for a in range(PASSES):
+                    quantize_wn(a)
+            if s == 3:
+                load_usual(7)
+                page.append(load_page(5))
+                page.append(load_page(6))
+                last_loads()
+                for hf in range(2):
+                    quantize_rows(h_q[0], h_t[0], half_cols(hf), staging("h_bf0%d" % hf))
+            if s == 7:
+                page.append(load_page(7))
+                for hf in range(2):
+                    quantize_rows(h_q[1], h_t[1], half_cols(hf), staging("h_bf1%d" % hf))
+            scatter_h(s, None)
+            if s == 7:
+                nc.gpsimd.tensor_copy(clock[:, 1:2], page[7][:, 0:1])
+            cols = first_pick(s - 2)[1]
+            floor_x(s - 2, cols, picked[s % 2][:, cols])
+            hf, cols = first_pick(s - 1)
+            gather_x(s - 1, hf, picked[(s - 1) % 2][:, cols])
+            if s == 5:
+                shared_bf = shared[:].bitcast(BF16)
+                for hf in range(2):
+                    stage = shared_bf[:, hf * PACK * HALF : (hf + 1) * PACK * HALF]
+                    quantize_rows(x_q[0], x_rows[0], half_cols(hf), stage)
+        floor_x(6, whole, picked[0][:, whole])
+        gather_x(7, None, picked[1][:])
+        lower, upper = picked[1][:, half_cols(0)], picked[1][:, half_cols(1)]
+        floor_x(7, half_cols(0), lower)
+        for u in range(2):
+            quantize_rows(x_q[1], x_rows[1], units[u], staging("x_bf1%d" % u))
+        floor_x(7, half_cols(1), upper)
+        gather_x(4, 1, lower)
+        gather_x(5, 1, upper)
+        floor_x(4, half_cols(1), lower)
+        gather_x(6, 1, lower)
+        floor_x(5, half_cols(1), upper)
+        floor_x(6, half_cols(1), lower)
+        quantize_rows(x_q[1], x_rows[1], units[2], staging("x_bf12"))
+
+        def products(bank, j0, lhs, rhs, widths):
+            n0 = 0
+            for width in widths:
+                for a in reversed(range(PASSES)):
+                    l_codes, l_scales = lhs(a, slice(j0, j0 + P))
+                    r_codes, r_scales = rhs(a, n0, width)
+                    nc.tensor.matmul_mx(
+                        out=bank[:, n0 : n0 + width], lhsT=l_codes, lhsT_scale=l_scales,
+                        rhs=r_codes, rhs_scale=r_scales, start=(a == PASSES - 1), stop=(a == 0),
+                    )
+                n0 = n0 + width
+
+        def v_op(a, cols):
+            return v_codes[a][:, cols].bitcast(FP8X4), v_scales[4 * a : P, cols]
+
+        def h_op(a, cols):
+            return h_q[a][0][:, cols].bitcast(FP8X4), h_q[a][1][:, cols]
+
+        def x_op(a, cols):
+            return x_q[a][0][:, cols].bitcast(FP8X4), x_q[a][1][:, cols]
+
+        def wn_op(a, n0, width):
+            cols = slice(a * N + n0, a * N + n0 + width)
+            return wn_q[0][:, cols].bitcast(FP8X4), wn_q[1][:, cols]
+
+        def wh_op(a, n0, width):
+            return wh_t[:, a, n0 : n0 + width].bitcast(FP8X4), wh_sc[:, a, n0 : n0 + width]
+
+        def wr_op(a, n0, width):
+            return wr_t[:, a, 2 * n0 : 2 * (n0 + width)].bitcast(FP4X4), wr_sc[:, a, n0 : n0 + width]
+
+        late_sides = ring.tile([P, BLOCKS, 2 * N], F32, name="late_sides", tag="big0", bufs=1)
+        sides = [usual_buf[jb][:, 0 : 2 * N] for jb in range(BLOCKS)] + [late_sides[:, jb, :] for jb in range(BLOCKS)]
+        for jb in range(2 * BLOCKS):
+            notes_bank = psum.tile([P, HALF], F32, name="notes_bank", tag="bank_u", bufs=2)
+            products(notes_bank, jb * P, v_op, wn_op, (256, 128))
+            nc.scalar.copy(sides[jb][:, 0:N], notes_bank[:, 0:N])
+        for jb in range(2 * BLOCKS):
+            state_bank = psum.tile([P, HALF], F32, name="state_bank", tag="bank_u", bufs=2)
+            products(state_bank, jb * P, h_op, wh_op, (256, 128))
+            nc.scalar.activation(sides[jb][:, N : 2 * N], state_bank[:, 0:N], ACT.Copy, scale=-1.0)
+
+        y_banks = [psum.tile([P, HALF], F32, name="y_bank%d" % i, tag="bank_h", bufs=4) for i in range(4)]
+        y_banks = y_banks + [psum.tile([P, HALF], F32, name="y_bank%d" % i, tag="bank_u", bufs=2) for i in (4, 5)]
+
+        def y_bank(nb, cols):
+            hf = cols.start // HALF
+            return y_banks[OUT_TILES * hf + nb][:, cols.start - hf * HALF : cols.stop - hf * HALF]
+
+        def combine(u):
+            unit = units[u]
+            for jb in range(unit.start // P, unit.stop // P):
+                recalled_bank = psum.tile([P, HALF], F32, name="recalled_bank", tag="bank_a", bufs=2)
+                products(recalled_bank, jb * P, x_op, wr_op, (128, 128, 128))
+                larger = work("larger")
+                nc.vector.tensor_tensor(larger[:, 0:N], recalled_bank[:, 0:N], sides[jb][:, 0:N], ALU.max)
+                for nb in range(OUT_TILES):
+                    n0 = nb * P
+                    add_transposed(y_bank(nb, slice(jb * P, (jb + 1) * P)), sides[jb][:, N + n0 : N + n0 + P], larger[:, n0 : n0 + P])
+
+        y_home = [sides[jb][:, 0:256] for jb in (0, 1, 4, 5, 6, 7)]
+        y_home = y_home + [usual_buf[nb][:, N : N + HALF] for nb in range(OUT_TILES)]
+
+        def put(u, nb):
+            unit = units[u]
+            y = y_home[OUT_TILES * u + nb]
+            nc.scalar.copy(y, y_bank(nb, unit))
+            nc.vector.tensor_tensor(
+                visit[nb][:].indirect(late["idx4"][:, unit.start // 16 : unit.stop // 16]),
+                y, late["wgo"][:, unit], ALU.mult,
+            )
+
+        combine(0)
+        put(0, 0)
+        nc.gpsimd.tensor_copy(clock[:, 0:1], visit[0][:, 0:1])
+        put(0, 1)
+        combine(1)
+        combine(2)
+        put(0, 2)
+        for nb in range(OUT_TILES):
+            put(1, nb)
+        for nb in range(OUT_TILES):
+            put(2, nb)
+            nc.sync.dma_start(out[nb * P : (nb + 1) * P, :], visit[nb][:])

@@ -68,10 +68,7 @@ def tile_list_visit_page_update_kernel(
             nc.sync.dma_start(usual_buf[s % 4][:], slice_rows(usual, s))
 
         def load_page(s):
-            if s == 7:
-                tile = ring.tile([P, T2], F32, name="page7", tag="last_page", bufs=1)
-            else:
-                tile = ring.tile([P, T2], F32, name="page%d" % s, tag="page", bufs=4)
+            tile = ring.tile([P, T2], F32, name="page%d" % s, tag="page", bufs=5)
             nc.sync.dma_start(tile[:], slice_rows(page0, s))
             return tile
 
@@ -103,6 +100,8 @@ def tile_list_visit_page_update_kernel(
         make_identity(nc, ident[:])
 
         w1_raw = {}
+        gain_t = kept([P, PASSES, PACK], F32, "gain_t")
+        nc.sync.dma_start(gain_t[:], gain.rearrange("(b p t) -> p b t", b=PASSES, t=PACK))
         scale_rows = ring.tile([P, T], U8, name="scale_rows", tag="staging", bufs=3, align_bytes=64)
         for q in range(4):
             nc.sync.dma_start(
@@ -114,21 +113,19 @@ def tile_list_visit_page_update_kernel(
         idx = load_list(offs, "idx")
         w1_raw[1, 0] = load_weight_rows(w1, 1, half_cols(0), "w1_raw10")
         table.append(load_table(1))
-        gain_t = kept([P, PASSES, PACK], F32, "gain_t")
-        nc.sync.dma_start(gain_t[:], gain.rearrange("(b p t) -> p b t", b=PASSES, t=PACK))
         idx2 = load_list(offs2, "idx2")
         load_usual(0)
         page = [load_page(0)]
         wgs_rows = wgs.rearrange("(i t) j -> i t j", t=PACK)
         wgs_first = kept([P, S], F32, "wgs_first")
-        for q in range(4):
+        for q in (0, 2, 1, 3):
             nc.sync.dma_start(wgs_first[32 * q : 32 * q + 32, :], wgs_rows[:, 0, :])
         load_usual(1)
         idx3 = load_list(offs3, "idx3")
         low_t = kept([P, PASSES, PACK], F32, "low_t")
         nc.sync.dma_start(low_t[:], low.rearrange("(b p t) -> p b t", b=PASSES, t=PACK))
         wgs_rest = kept([P, PACK - 1, S], F32, "wgs_rest")
-        for q in range(4):
+        for q in (0, 2, 1, 3):
             nc.sync.dma_start(wgs_rest[32 * q : 32 * q + 32, :, :], wgs_rows[:, 1:PACK, :])
         page.append(load_page(1))
         w1_raw[0, 1] = load_weight_rows(w1, 0, half_cols(1), "w1_raw01")
@@ -172,8 +169,8 @@ def tile_list_visit_page_update_kernel(
         def cast_w1(a, b, copy):
             stage = staging("w1_bf%d%d" % (a, b))
             copy(
-                stage[:].rearrange("p (t m j) -> p m j t", t=PACK, j=PACK),
-                w1_raw[a, b][:].rearrange("p j (m t) -> p m j t", t=PACK),
+                stage[:].rearrange("p (t m j) -> p m t j", t=PACK, j=PACK),
+                w1_raw[a, b][:].rearrange("p j (m t) -> p m t j", t=PACK),
             )
             return stage
 
@@ -238,10 +235,8 @@ def tile_list_visit_page_update_kernel(
                         start=(a == 0),
                         stop=(a == PASSES - 1),
                     )
-            if s == 5:
-                logs = shared[:, (1 - hf) * S : (1 - hf) * S + HALF]
-            elif s == 7 and hf == 1:
-                logs = ring.tile([P, HALF], F32, name="logs_last", tag="last_page", bufs=1)[:]
+            if s >= 6 and hf == 0:
+                logs = shared[:, (7 - s) * S : (7 - s) * S + HALF]
             else:
                 logs = work("logs")[:]
             nc.scalar.activation(logs, a_bank[:], ACT.Abs)
@@ -251,6 +246,27 @@ def tile_list_visit_page_update_kernel(
                 cols = slice(jb * P, (jb + 1) * P)
                 add_transposed(h_bank[:, cols], neg_usual[:, cols], logs[:, cols])
             nc.scalar.activation(h_t[b][:, t, half_cols(hf)], h_bank[:], ACT.Copy, scale=gain_t[:, b, t : t + 1])
+
+        def make_first_h():
+            h_t[0] = ring.tile([P, PACK, S], F32, name="h0", tag="big0", bufs=1)
+            a_bank = psum.tile([P, HALF], F32, name="a_first", tag="bank_a", bufs=2)
+            for a in range(PASSES):
+                codes, scales = w1_q[a, 0]
+                nc.tensor.matmul_mx(
+                    out=a_bank[:],
+                    lhsT=codes[:, 0:P].bitcast(FP8X4),
+                    lhsT_scale=scales[:, 0:P],
+                    rhs=v_codes[a][:, whole].bitcast(FP8X4),
+                    rhs_scale=v_scales[4 * a : P, whole],
+                    start=(a == 0),
+                    stop=(a == PASSES - 1),
+                )
+            logs = work("logs_first")
+            nc.scalar.activation(logs[:], a_bank[:], ACT.Abs)
+            nc.scalar.activation(logs[:], logs[:], ACT.Ln, bias=1.0)
+            diff = work("diff_first")
+            nc.vector.tensor_tensor(diff[:], logs[:], usual_buf[0][:, whole], ALU.subtract)
+            nc.vector.tensor_scalar(h_t[0][:, 0, whole], diff[:], gain_t[:, 0, 0:1], None, op0=ALU.mult)
 
         def scatter_h(s, hf):
             b, t = divmod(s, PACK)
@@ -288,69 +304,7 @@ def tile_list_visit_page_update_kernel(
             quantize(wn_q, slice(a * N, a * N + 256), stage[:, 0:1024])
             quantize(wn_q, slice(a * N + 256, (a + 1) * N), stage[:, 1024 : PACK * N])
 
-        def first_pick(s):
-            return (None, slice(0, S)) if s < PACK else (0, whole)
-
         units = [slice(0, 256), slice(256, 512), slice(512, 1024)]
-
-        clock = kept([P, 8], F32, "clock")
-        make_h(0, 0)
-        scatter_h(0, 0)
-        make_h(0, 1)
-        scatter_h(0, 1)
-        load_usual(4)
-        page.append(load_page(4))
-        for hf in range(2):
-            make_h(1, hf)
-        load_usual(5)
-        scatter_h(1, None)
-        gather_x(0, None, picked[0][:])
-        for a in range(PASSES):
-            quantize(w1_q[a, 1], whole, cast_w1(a, 1, nc.scalar.copy)[:])
-        for s in range(2, 8):
-            for hf in range(2):
-                make_h(s, hf)
-            if s == 2:
-                load_usual(6)
-                for a in range(PASSES):
-                    quantize_wn(a)
-            if s == 3:
-                load_usual(7)
-                page.append(load_page(5))
-                page.append(load_page(6))
-                last_loads()
-                for hf in range(2):
-                    quantize_rows(h_q[0], h_t[0], half_cols(hf), staging("h_bf0%d" % hf))
-            if s == 7:
-                page.append(load_page(7))
-                for hf in range(2):
-                    quantize_rows(h_q[1], h_t[1], half_cols(hf), staging("h_bf1%d" % hf))
-            scatter_h(s, None)
-            if s == 7:
-                nc.gpsimd.tensor_copy(clock[:, 1:2], page[7][:, 0:1])
-            cols = first_pick(s - 2)[1]
-            floor_x(s - 2, cols, picked[s % 2][:, cols])
-            hf, cols = first_pick(s - 1)
-            gather_x(s - 1, hf, picked[(s - 1) % 2][:, cols])
-            if s == 5:
-                shared_bf = shared[:].bitcast(BF16)
-                for hf in range(2):
-                    stage = shared_bf[:, hf * PACK * HALF : (hf + 1) * PACK * HALF]
-                    quantize_rows(x_q[0], x_rows[0], half_cols(hf), stage)
-        floor_x(6, whole, picked[0][:, whole])
-        gather_x(7, None, picked[1][:])
-        lower, upper = picked[1][:, half_cols(0)], picked[1][:, half_cols(1)]
-        floor_x(7, half_cols(0), lower)
-        for u in range(2):
-            quantize_rows(x_q[1], x_rows[1], units[u], staging("x_bf1%d" % u))
-        floor_x(7, half_cols(1), upper)
-        gather_x(4, 1, lower)
-        gather_x(5, 1, upper)
-        floor_x(4, half_cols(1), lower)
-        gather_x(6, 1, lower)
-        floor_x(5, half_cols(1), upper)
-        floor_x(6, half_cols(1), lower)
-        quantize_rows(x_q[1], x_rows[1], units[2], staging("x_bf12"))
 
         def products(bank, j0, lhs, rhs, widths):
             n0 = 0
@@ -383,19 +337,95 @@ def tile_list_visit_page_update_kernel(
         def wr_op(a, n0, width):
             return wr_t[:, a, 2 * n0 : 2 * (n0 + width)].bitcast(FP4X4), wr_sc[:, a, n0 : n0 + width]
 
+        make_first_h()
+        scatter_h(0, 0)
+        make_h(0, 1)
+        scatter_h(0, 1)
+        load_usual(4)
+        page.append(load_page(4))
+        for hf in range(2):
+            make_h(1, hf)
+        load_usual(5)
+        scatter_h(1, None)
+        gather_x(0, None, picked[0][:])
+        for a in range(PASSES):
+            quantize(w1_q[a, 1], whole, cast_w1(a, 1, nc.scalar.copy)[:])
+        for s in (2, 3):
+            for hf in range(2):
+                make_h(s, hf)
+            load_usual(s + 4)
+            if s == 2:
+                for a in range(PASSES):
+                    quantize_wn(a)
+            scatter_h(s, None)
+            floor_x(s - 2, slice(0, S), picked[s % 2][:])
+            gather_x(s - 1, None, picked[(s - 1) % 2][:])
+        for s in range(5, 8):
+            page.append(load_page(s))
+        last_loads()
+        for hf in range(2):
+            quantize_rows(h_q[0], h_t[0], half_cols(hf), staging("h_bf0%d" % hf))
+        make_h(4, 0)
+        scatter_h(4, 0)
+        floor_x(2, slice(0, S), picked[0][:])
+        gather_x(3, None, picked[1][:])
+        make_h(5, 0)
+        scatter_h(5, 0)
+        floor_x(3, slice(0, S), picked[1][:])
+        for s in (6, 7):
+            make_h(s, 0)
+            scatter_h(s, 0)
+        quantize_rows(h_q[1], h_t[1], half_cols(0), staging("h_bf10"))
+        shared_bf = shared[:].bitcast(BF16)
+        for hf in range(2):
+            stage = shared_bf[:, hf * PACK * HALF : (hf + 1) * PACK * HALF]
+            quantize_rows(x_q[0], x_rows[0], half_cols(hf), stage)
+
+        def spent_wgs(s):
+            return wgs_slice(s + 1 - PACK)[:, half_cols(1)]
+
+        for s in range(4, 8):
+            make_h(s, 1)
+            scatter_h(s, 1)
+            if s in (5, 6):
+                gather_x(s - 1, 0, spent_wgs(s - 1))
+                floor_x(s - 1, whole, spent_wgs(s - 1))
+        quantize_rows(h_q[1], h_t[1], half_cols(1), staging("h_bf11"))
         late_sides = ring.tile([P, BLOCKS, 2 * N], F32, name="late_sides", tag="big0", bufs=1)
         sides = [usual_buf[jb][:, 0 : 2 * N] for jb in range(BLOCKS)] + [late_sides[:, jb, :] for jb in range(BLOCKS)]
-        for jb in range(2 * BLOCKS):
+
+        def make_notes(jb):
             notes_bank = psum.tile([P, HALF], F32, name="notes_bank", tag="bank_u", bufs=2)
             products(notes_bank, jb * P, v_op, wn_op, (256, 128))
             nc.scalar.copy(sides[jb][:, 0:N], notes_bank[:, 0:N])
-        for jb in range(2 * BLOCKS):
+
+        def make_state(jb):
             state_bank = psum.tile([P, HALF], F32, name="state_bank", tag="bank_u", bufs=2)
             products(state_bank, jb * P, h_op, wh_op, (256, 128))
             nc.scalar.activation(sides[jb][:, N : 2 * N], state_bank[:, 0:N], ACT.Copy, scale=-1.0)
 
+        for jb in range(BLOCKS):
+            make_notes(jb)
+            make_state(jb)
+        for jb in range(BLOCKS, 2 * BLOCKS):
+            make_notes(jb)
+        gather_x(6, 0, spent_wgs(6))
+        gather_x(7, 0, picked[0][:, whole])
+        floor_x(6, whole, spent_wgs(6))
+        floor_x(7, whole, picked[0][:, whole])
+        for u in range(2):
+            quantize_rows(x_q[1], x_rows[1], units[u], staging("x_bf1%d" % u))
+        gather_x(4, 1, spent_wgs(6))
+        gather_x(5, 1, picked[0][:, whole])
+        floor_x(4, half_cols(1), spent_wgs(6))
+        gather_x(6, 1, spent_wgs(6))
+        floor_x(5, half_cols(1), picked[0][:, whole])
+        gather_x(7, 1, picked[0][:, whole])
+        floor_x(6, half_cols(1), spent_wgs(6))
+        floor_x(7, half_cols(1), picked[0][:, whole])
+        quantize_rows(x_q[1], x_rows[1], units[2], staging("x_bf12"))
+
         y_banks = [psum.tile([P, HALF], F32, name="y_bank%d" % i, tag="bank_h", bufs=4) for i in range(4)]
-        y_banks = y_banks + [psum.tile([P, HALF], F32, name="y_bank%d" % i, tag="bank_u", bufs=2) for i in (4, 5)]
 
         def y_bank(nb, cols):
             hf = cols.start // HALF
@@ -426,9 +456,11 @@ def tile_list_visit_page_update_kernel(
 
         combine(0)
         put(0, 0)
-        nc.gpsimd.tensor_copy(clock[:, 0:1], visit[0][:, 0:1])
         put(0, 1)
         combine(1)
+        for jb in range(BLOCKS, 2 * BLOCKS):
+            make_state(jb)
+        y_banks.extend([psum.tile([P, HALF], F32, name="y_bank%d" % i, tag="bank_u", bufs=2) for i in (4, 5)])
         combine(2)
         put(0, 2)
         for nb in range(OUT_TILES):

@@ -25,6 +25,8 @@ HALF = 512
 BLOCKS = HALF // P
 OUT_TILES = N // P
 LIST_COLS = S // 16
+LEAD = 256
+DIRECT = []
 
 
 def tile_list_visit_page_update_kernel(
@@ -100,8 +102,7 @@ def tile_list_visit_page_update_kernel(
         make_identity(nc, ident[:])
 
         w1_raw = {}
-        gain_t = kept([P, PASSES, PACK], F32, "gain_t")
-        nc.sync.dma_start(gain_t[:], gain.rearrange("(b p t) -> p b t", b=PASSES, t=PACK))
+        idx = load_list(offs, "idx")
         scale_rows = ring.tile([P, T], U8, name="scale_rows", tag="staging", bufs=3, align_bytes=64)
         for q in range(4):
             nc.sync.dma_start(
@@ -110,31 +111,40 @@ def tile_list_visit_page_update_kernel(
             )
         w1_raw[0, 0] = load_weight_rows(w1, 0, half_cols(0), "w1_raw00")
         table = [load_table(0)]
-        idx = load_list(offs, "idx")
         w1_raw[1, 0] = load_weight_rows(w1, 1, half_cols(0), "w1_raw10")
         table.append(load_table(1))
+        gain_t = kept([P, PASSES, PACK], F32, "gain_t")
+        nc.sync.dma_start(gain_t[:], gain.rearrange("(b p t) -> p b t", b=PASSES, t=PACK))
         idx2 = load_list(offs2, "idx2")
-        load_usual(0)
+        lead = slice(0, LEAD)
+        rest = slice(LEAD, S)
+        nc.sync.dma_start(usual_buf[0][:, lead], slice_rows(usual, 0)[:, lead])
         page = [load_page(0)]
         wgs_rows = wgs.rearrange("(i t) j -> i t j", t=PACK)
-        wgs_first = kept([P, S], F32, "wgs_first")
-        for q in (0, 2, 1, 3):
-            nc.sync.dma_start(wgs_first[32 * q : 32 * q + 32, :], wgs_rows[:, 0, :])
+        wgs_t = [kept([P, S], F32, "wgs%d" % t) for t in range(PACK)]
+
+        def load_wgs(t, cols=slice(0, S)):
+            for q in (0, 2, 1, 3):
+                nc.sync.dma_start(wgs_t[t][32 * q : 32 * q + 32, cols], wgs_rows[:, t, cols])
+
+        load_wgs(0, lead)
+        nc.sync.dma_start(usual_buf[0][:, rest], slice_rows(usual, 0)[:, rest])
+        load_wgs(0, rest)
         load_usual(1)
         idx3 = load_list(offs3, "idx3")
         low_t = kept([P, PASSES, PACK], F32, "low_t")
         nc.sync.dma_start(low_t[:], low.rearrange("(b p t) -> p b t", b=PASSES, t=PACK))
-        wgs_rest = kept([P, PACK - 1, S], F32, "wgs_rest")
-        for q in (0, 2, 1, 3):
-            nc.sync.dma_start(wgs_rest[32 * q : 32 * q + 32, :, :], wgs_rows[:, 1:PACK, :])
+        load_wgs(1)
         page.append(load_page(1))
+        load_usual(2)
         w1_raw[0, 1] = load_weight_rows(w1, 0, half_cols(1), "w1_raw01")
         w1_raw[1, 1] = load_weight_rows(w1, 1, half_cols(1), "w1_raw11")
-        load_usual(2)
-        page.append(load_page(2))
-        wn_raw = [load_weight_rows(wn, a, slice(0, N), "wn_raw%d" % a) for a in range(PASSES)]
         load_usual(3)
+        load_wgs(2)
+        page.append(load_page(2))
+        load_wgs(3)
         page.append(load_page(3))
+        wn_raw = [load_weight_rows(wn, a, slice(0, N), "wn_raw%d" % a) for a in range(PASSES)]
         wr_t = kept([P, PASSES, 2 * N], U8, "wr_t")
         wh_t = kept([P, PASSES, N], U32, "wh_t")
         late = {}
@@ -154,7 +164,7 @@ def tile_list_visit_page_update_kernel(
                 visit.append(tile)
 
         def wgs_slice(t):
-            return wgs_first[:] if t == 0 else wgs_rest[:, t - 1, :]
+            return wgs_t[t][:]
 
         def staging(name):
             return ring.tile([P, PACK * HALF], BF16, name=name, tag="staging", bufs=3, align_bytes=64)
@@ -177,8 +187,8 @@ def tile_list_visit_page_update_kernel(
         def interleave(src, stage):
             width = src.shape[2]
             nc.scalar.copy(
-                stage[:, 0 : PACK * width].rearrange("p (c i t) -> p c t i", i=4, t=PACK),
-                src.rearrange("p t (c i) -> p c t i", i=4),
+                stage[:, 0 : PACK * width].rearrange("p (c t) -> p c t", t=PACK),
+                src.rearrange("p t c -> p c t"),
             )
             return stage
 
@@ -209,12 +219,42 @@ def tile_list_visit_page_update_kernel(
             nc.vector.tensor_copy(v_codes[1][:, half_cols(hf)], table[1][:].indirect(half_list(idx, hf)))
 
         h_t = {}
+        picked = [kept([P, S], F32, "picked%d" % i) for i in range(2)]
         shared = kept([P, 2 * S], F32, "shared")
+
+        def make_direct_h(s, hf):
+            b, t = divmod(s, PACK)
+            cols = half_cols(hf)
+            gain_col = gain_t[:, b, t : t + 1]
+            scaled = usual_buf[s % 4][:, cols]
+            nc.scalar.activation(scaled, scaled, ACT.Copy, scale=gain_col)
+            a_bank = psum.tile([P, HALF], F32, name="a_direct", tag="bank_a", bufs=2)
+            for a in range(PASSES):
+                codes, scales = w1_q[a, b]
+                nc.tensor.matmul_mx(
+                    out=a_bank[:],
+                    lhsT=codes[:, t * P : (t + 1) * P].bitcast(FP8X4),
+                    lhsT_scale=scales[:, t * P : (t + 1) * P],
+                    rhs=v_codes[a][:, cols].bitcast(FP8X4),
+                    rhs_scale=v_scales[4 * a : P, cols],
+                    start=(a == 0),
+                    stop=(a == PASSES - 1),
+                )
+            if (s, hf) in [(6, 1), (7, 1)]:
+                logs = shared[:, [(6, 1), (7, 1)].index((s, hf)) * S :][:, whole]
+            else:
+                logs = work("logs")[:]
+            nc.scalar.activation(logs, a_bank[:], ACT.Abs)
+            nc.scalar.activation(logs, logs, ACT.Ln, bias=1.0)
+            nc.vector.scalar_tensor_tensor(h_t[b][:, t, cols], logs, gain_col, scaled, ALU.mult, ALU.subtract)
 
         def make_h(s, hf):
             b, t = divmod(s, PACK)
             if b not in h_t:
                 h_t[b] = ring.tile([P, PACK, S], F32, name="h%d" % b, tag="big%d" % b, bufs=1)
+            if (s, hf) in DIRECT:
+                make_direct_h(s, hf)
+                return
             usual_bank = psum.tile([P, HALF], F32, name="usual_bank", tag="bank_u", bufs=2)
             for jb in range(BLOCKS):
                 j0 = hf * HALF + jb * P
@@ -235,8 +275,10 @@ def tile_list_visit_page_update_kernel(
                         start=(a == 0),
                         stop=(a == PASSES - 1),
                     )
-            if s >= 6 and hf == 0:
-                logs = shared[:, (7 - s) * S : (7 - s) * S + HALF]
+            if (s, hf) in [(6, 1), (7, 1)]:
+                logs = shared[:, [(6, 1), (7, 1)].index((s, hf)) * S :][:, whole]
+            elif (s, hf) == (4, 1):
+                logs = picked[1][:, whole]
             else:
                 logs = work("logs")[:]
             nc.scalar.activation(logs, a_bank[:], ACT.Abs)
@@ -247,26 +289,30 @@ def tile_list_visit_page_update_kernel(
                 add_transposed(h_bank[:, cols], neg_usual[:, cols], logs[:, cols])
             nc.scalar.activation(h_t[b][:, t, half_cols(hf)], h_bank[:], ACT.Copy, scale=gain_t[:, b, t : t + 1])
 
-        def make_first_h():
-            h_t[0] = ring.tile([P, PACK, S], F32, name="h0", tag="big0", bufs=1)
+        def make_first_h(cols):
+            width = cols.stop - cols.start
             a_bank = psum.tile([P, HALF], F32, name="a_first", tag="bank_a", bufs=2)
             for a in range(PASSES):
                 codes, scales = w1_q[a, 0]
                 nc.tensor.matmul_mx(
-                    out=a_bank[:],
+                    out=a_bank[:, 0:width],
                     lhsT=codes[:, 0:P].bitcast(FP8X4),
                     lhsT_scale=scales[:, 0:P],
-                    rhs=v_codes[a][:, whole].bitcast(FP8X4),
-                    rhs_scale=v_scales[4 * a : P, whole],
+                    rhs=v_codes[a][:, cols].bitcast(FP8X4),
+                    rhs_scale=v_scales[4 * a : P, cols],
                     start=(a == 0),
                     stop=(a == PASSES - 1),
                 )
-            logs = work("logs_first")
-            nc.scalar.activation(logs[:], a_bank[:], ACT.Abs)
-            nc.scalar.activation(logs[:], logs[:], ACT.Ln, bias=1.0)
-            diff = work("diff_first")
-            nc.vector.tensor_tensor(diff[:], logs[:], usual_buf[0][:, whole], ALU.subtract)
-            nc.vector.tensor_scalar(h_t[0][:, 0, whole], diff[:], gain_t[:, 0, 0:1], None, op0=ALU.mult)
+            logs = work("logs_first")[:, 0:width]
+            nc.scalar.activation(logs, a_bank[:, 0:width], ACT.Abs)
+            nc.scalar.activation(logs, logs, ACT.Ln, bias=1.0)
+            diff = work("diff_first")[:, 0:width]
+            nc.vector.tensor_tensor(diff, logs, usual_buf[0][:, cols], ALU.subtract)
+            nc.vector.tensor_scalar(h_t[0][:, 0, cols], diff, gain_t[:, 0, 0:1], None, op0=ALU.mult)
+            nc.vector.tensor_tensor(
+                page[0][:].indirect(idx2[:, cols.start // 16 : cols.stop // 16]), h_t[0][:, 0, cols],
+                wgs_t[0][:, cols], ALU.mult,
+            )
 
         def scatter_h(s, hf):
             b, t = divmod(s, PACK)
@@ -278,7 +324,6 @@ def tile_list_visit_page_update_kernel(
                     wgs_slice(t)[:, half_cols(hf)], ALU.mult,
                 )
 
-        picked = [kept([P, S], F32, "picked%d" % i) for i in range(2)]
         x_rows = [kept([P, PACK, S], BF16, "x_rows%d" % b) for b in range(PASSES)]
 
         def gather_x(s, hf, dst):
@@ -300,7 +345,7 @@ def tile_list_visit_page_update_kernel(
             quantize(operand, cols, stage[:, 0 : PACK * (cols.stop - cols.start)])
 
         def quantize_wn(a):
-            stage = interleave(wn_raw[a][:], staging("wn_bf%d" % a))
+            stage = interleave(wn_raw[a][:], shared[:, a * S : (a + 1) * S].bitcast(BF16))
             quantize(wn_q, slice(a * N, a * N + 256), stage[:, 0:1024])
             quantize(wn_q, slice(a * N + 256, (a + 1) * N), stage[:, 1024 : PACK * N])
 
@@ -337,10 +382,9 @@ def tile_list_visit_page_update_kernel(
         def wr_op(a, n0, width):
             return wr_t[:, a, 2 * n0 : 2 * (n0 + width)].bitcast(FP4X4), wr_sc[:, a, n0 : n0 + width]
 
-        make_first_h()
-        scatter_h(0, 0)
-        make_h(0, 1)
-        scatter_h(0, 1)
+        h_t[0] = ring.tile([P, PACK, S], F32, name="h0", tag="big0", bufs=1)
+        for cols in (slice(0, 256), slice(256, 512), slice(512, 1024)):
+            make_first_h(cols)
         load_usual(4)
         page.append(load_page(4))
         for hf in range(2):
@@ -348,41 +392,60 @@ def tile_list_visit_page_update_kernel(
         load_usual(5)
         scatter_h(1, None)
         gather_x(0, None, picked[0][:])
-        for a in range(PASSES):
-            quantize(w1_q[a, 1], whole, cast_w1(a, 1, nc.scalar.copy)[:])
         for s in (2, 3):
             for hf in range(2):
                 make_h(s, hf)
             load_usual(s + 4)
             if s == 2:
                 for a in range(PASSES):
-                    quantize_wn(a)
+                    quantize(w1_q[a, 1], whole, cast_w1(a, 1, nc.scalar.copy)[:])
             scatter_h(s, None)
             floor_x(s - 2, slice(0, S), picked[s % 2][:])
             gather_x(s - 1, None, picked[(s - 1) % 2][:])
         for s in range(5, 8):
             page.append(load_page(s))
         last_loads()
-        for hf in range(2):
-            quantize_rows(h_q[0], h_t[0], half_cols(hf), staging("h_bf0%d" % hf))
+        shared_bf = shared[:].bitcast(BF16)
+
+        def quantize_x0(hf):
+            stage = shared_bf[:, hf * PACK * HALF : (hf + 1) * PACK * HALF]
+            quantize_rows(x_q[0], x_rows[0], half_cols(hf), stage)
+
+        quantize_rows(h_q[0], h_t[0], half_cols(0), staging("h_bf00"))
         make_h(4, 0)
         scatter_h(4, 0)
         floor_x(2, slice(0, S), picked[0][:])
         gather_x(3, None, picked[1][:])
+        quantize_rows(h_q[0], h_t[0], half_cols(1), staging("h_bf01"))
         make_h(5, 0)
         scatter_h(5, 0)
         floor_x(3, slice(0, S), picked[1][:])
         for s in (6, 7):
+            quantize_wn(s - 6)
             make_h(s, 0)
             scatter_h(s, 0)
-        quantize_rows(h_q[1], h_t[1], half_cols(0), staging("h_bf10"))
-        shared_bf = shared[:].bitcast(BF16)
-        for hf in range(2):
-            stage = shared_bf[:, hf * PACK * HALF : (hf + 1) * PACK * HALF]
-            quantize_rows(x_q[0], x_rows[0], half_cols(hf), stage)
 
         def spent_wgs(s):
             return wgs_slice(s + 1 - PACK)[:, half_cols(1)]
+
+        notes = ring.tile([P, OUT_TILES, S], F32, name="notes", tag="big0", bufs=1)
+
+        def natural(bank, nb, cols, weight, data):
+            for a in reversed(range(PASSES)):
+                w_codes, w_scales = weight(a, nb * P, P)
+                d_codes, d_scales = data(a, cols)
+                nc.tensor.matmul_mx(
+                    out=bank, lhsT=w_codes, lhsT_scale=w_scales, rhs=d_codes, rhs_scale=d_scales,
+                    start=(a == PASSES - 1), stop=(a == 0),
+                )
+
+        def make_notes(i):
+            if i >= 2 * OUT_TILES:
+                return
+            hf, nb = divmod(i, OUT_TILES)
+            notes_bank = psum.tile([P, HALF], F32, name="notes_bank", tag="bank_u", bufs=2)
+            natural(notes_bank[:], nb, half_cols(hf), wn_op, v_op)
+            nc.scalar.copy(notes[:, nb, half_cols(hf)], notes_bank[:])
 
         for s in range(4, 8):
             make_h(s, 1)
@@ -390,81 +453,54 @@ def tile_list_visit_page_update_kernel(
             if s in (5, 6):
                 gather_x(s - 1, 0, spent_wgs(s - 1))
                 floor_x(s - 1, whole, spent_wgs(s - 1))
+            if s == 4:
+                quantize_rows(h_q[1], h_t[1], half_cols(0), picked[1][:].bitcast(BF16))
+            if (s, 1) in [(6, 1), (7, 1)]:
+                quantize_x0([(6, 1), (7, 1)].index((s, 1)))
+            for jb in ():
+                make_notes(jb)
         quantize_rows(h_q[1], h_t[1], half_cols(1), staging("h_bf11"))
-        late_sides = ring.tile([P, BLOCKS, 2 * N], F32, name="late_sides", tag="big0", bufs=1)
-        sides = [usual_buf[jb][:, 0 : 2 * N] for jb in range(BLOCKS)] + [late_sides[:, jb, :] for jb in range(BLOCKS)]
-
-        def make_notes(jb):
-            notes_bank = psum.tile([P, HALF], F32, name="notes_bank", tag="bank_u", bufs=2)
-            products(notes_bank, jb * P, v_op, wn_op, (256, 128))
-            nc.scalar.copy(sides[jb][:, 0:N], notes_bank[:, 0:N])
-
-        def make_state(jb):
-            state_bank = psum.tile([P, HALF], F32, name="state_bank", tag="bank_u", bufs=2)
-            products(state_bank, jb * P, h_op, wh_op, (256, 128))
-            nc.scalar.activation(sides[jb][:, N : 2 * N], state_bank[:, 0:N], ACT.Copy, scale=-1.0)
-
-        for jb in range(BLOCKS):
-            make_notes(jb)
-            make_state(jb)
-        for jb in range(BLOCKS, 2 * BLOCKS):
-            make_notes(jb)
+        for i in range(2 * OUT_TILES):
+            make_notes(i)
         gather_x(6, 0, spent_wgs(6))
         gather_x(7, 0, picked[0][:, whole])
         floor_x(6, whole, spent_wgs(6))
         floor_x(7, whole, picked[0][:, whole])
+        x_stage = [staging("x_bf1%d" % u) for u in range(2)]
         for u in range(2):
-            quantize_rows(x_q[1], x_rows[1], units[u], staging("x_bf1%d" % u))
-        gather_x(4, 1, spent_wgs(6))
-        gather_x(5, 1, picked[0][:, whole])
-        floor_x(4, half_cols(1), spent_wgs(6))
-        gather_x(6, 1, spent_wgs(6))
-        floor_x(5, half_cols(1), picked[0][:, whole])
-        gather_x(7, 1, picked[0][:, whole])
-        floor_x(6, half_cols(1), spent_wgs(6))
-        floor_x(7, half_cols(1), picked[0][:, whole])
+            quantize_rows(x_q[1], x_rows[1], units[u], x_stage[u])
+        last_picks = [spent_wgs(6), picked[0][:, whole]] + [x_stage[u][:].bitcast(F32)[:, whole] for u in range(2)]
+        gather_x(4, 1, last_picks[0])
+        gather_x(5, 1, last_picks[1])
+        floor_x(4, half_cols(1), last_picks[0])
+        gather_x(6, 1, last_picks[2])
+        floor_x(5, half_cols(1), last_picks[1])
+        gather_x(7, 1, last_picks[3])
+        floor_x(6, half_cols(1), last_picks[2])
+        floor_x(7, half_cols(1), last_picks[3])
         quantize_rows(x_q[1], x_rows[1], units[2], staging("x_bf12"))
-
-        y_banks = [psum.tile([P, HALF], F32, name="y_bank%d" % i, tag="bank_h", bufs=4) for i in range(4)]
-
-        def y_bank(nb, cols):
-            hf = cols.start // HALF
-            return y_banks[OUT_TILES * hf + nb][:, cols.start - hf * HALF : cols.stop - hf * HALF]
-
-        def combine(u):
-            unit = units[u]
-            for jb in range(unit.start // P, unit.stop // P):
-                recalled_bank = psum.tile([P, HALF], F32, name="recalled_bank", tag="bank_a", bufs=2)
-                products(recalled_bank, jb * P, x_op, wr_op, (128, 128, 128))
-                larger = work("larger")
-                nc.vector.tensor_tensor(larger[:, 0:N], recalled_bank[:, 0:N], sides[jb][:, 0:N], ALU.max)
-                for nb in range(OUT_TILES):
-                    n0 = nb * P
-                    add_transposed(y_bank(nb, slice(jb * P, (jb + 1) * P)), sides[jb][:, N + n0 : N + n0 + P], larger[:, n0 : n0 + P])
-
-        y_home = [sides[jb][:, 0:256] for jb in (0, 1, 4, 5, 6, 7)]
-        y_home = y_home + [usual_buf[nb][:, N : N + HALF] for nb in range(OUT_TILES)]
 
         def put(u, nb):
             unit = units[u]
-            y = y_home[OUT_TILES * u + nb]
-            nc.scalar.copy(y, y_bank(nb, unit))
+            width = unit.stop - unit.start
+            state_bank = psum.tile([P, HALF], F32, name="state_bank", tag="bank_h", bufs=4)
+            natural(state_bank[:, 0:width], nb, unit, wh_op, h_op)
+            recalled_bank = psum.tile([P, HALF], F32, name="recalled_bank", tag="bank_a", bufs=2)
+            step = HALF if width == HALF else P
+            for c0 in range(0, width, step):
+                piece = slice(unit.start + c0, unit.start + c0 + step)
+                natural(recalled_bank[:, c0 : c0 + step], nb, piece, wr_op, x_op)
+            larger = work("larger")[:, 0:width]
+            nc.vector.tensor_tensor(larger, recalled_bank[:, 0:width], notes[:, nb, unit], ALU.max)
+            y = work("y")[:, 0:width]
+            nc.vector.tensor_tensor(y, larger, state_bank[:, 0:width], ALU.subtract)
             nc.vector.tensor_tensor(
                 visit[nb][:].indirect(late["idx4"][:, unit.start // 16 : unit.stop // 16]),
                 y, late["wgo"][:, unit], ALU.mult,
             )
 
-        combine(0)
-        put(0, 0)
-        put(0, 1)
-        combine(1)
-        for jb in range(BLOCKS, 2 * BLOCKS):
-            make_state(jb)
-        y_banks.extend([psum.tile([P, HALF], F32, name="y_bank%d" % i, tag="bank_u", bufs=2) for i in (4, 5)])
-        combine(2)
-        put(0, 2)
-        for nb in range(OUT_TILES):
-            put(1, nb)
-        for nb in range(OUT_TILES):
-            put(2, nb)
-            nc.sync.dma_start(out[nb * P : (nb + 1) * P, :], visit[nb][:])
+        for u in range(len(units)):
+            for nb in range(OUT_TILES):
+                put(u, nb)
+                if u == len(units) - 1:
+                    nc.sync.dma_start(out[nb * P : (nb + 1) * P, :], visit[nb][:])

@@ -106,12 +106,17 @@ def tile_list_visit_page_update_kernel(
         scale_rows = ring.tile([P, T], U8, name="scale_rows", tag="staging", bufs=3, align_bytes=64)
         for q in range(4):
             nc.sync.dma_start(
-                scale_rows[32 * q : 32 * q + 8, :].bitcast(I32),
-                tab_scales[:, 4 * q : 4 * q + 4, :].bitcast(I32),
+                scale_rows[32 * q : 32 * q + 4, :].bitcast(I32),
+                tab_scales[0, 4 * q : 4 * q + 4, :].bitcast(I32),
             )
         w1_raw[0, 0] = load_weight_rows(w1, 0, half_cols(0), "w1_raw00")
         table = [load_table(0)]
         w1_raw[1, 0] = load_weight_rows(w1, 1, half_cols(0), "w1_raw10")
+        for q in range(4):
+            nc.sync.dma_start(
+                table_scales[32 * q + 4 : 32 * q + 8, :].bitcast(I32),
+                tab_scales[1, 4 * q : 4 * q + 4, :].bitcast(I32),
+            )
         table.append(load_table(1))
         gain_t = kept([P, PASSES, PACK], F32, "gain_t")
         nc.sync.dma_start(gain_t[:], gain.rearrange("(b p t) -> p b t", b=PASSES, t=PACK))
@@ -184,12 +189,13 @@ def tile_list_visit_page_update_kernel(
             )
             return stage
 
-        def interleave(src, stage):
+        def interleave(src, stage, negate=False):
             width = src.shape[2]
-            nc.scalar.copy(
-                stage[:, 0 : PACK * width].rearrange("p (c t) -> p c t", t=PACK),
-                src.rearrange("p t c -> p c t"),
-            )
+            dst = stage[:, 0 : PACK * width].rearrange("p (c t) -> p c t", t=PACK)
+            if negate:
+                nc.scalar.activation(dst, src.rearrange("p t c -> p c t"), ACT.Copy, scale=-1.0)
+            else:
+                nc.scalar.copy(dst, src.rearrange("p t c -> p c t"))
             return stage
 
         def work(name):
@@ -208,12 +214,12 @@ def tile_list_visit_page_update_kernel(
         whole = slice(0, HALF)
         stage = cast_w1(0, 0, nc.vector.tensor_copy)
         for q in range(4):
-            rows = slice(32 * q, 32 * q + 8)
+            rows = slice(32 * q, 32 * q + 4)
             nc.vector.tensor_copy(table_scales[rows, :].bitcast(I32), scale_rows[rows, :].bitcast(I32))
         nc.vector.tensor_copy(v_scales[:], table_scales[:].indirect(idx[:]))
         quantize(w1_q[0, 0], whole, stage[:])
         nc.vector.tensor_copy(v_codes[0][:], table[0][:].indirect(idx[:]))
-        stage = cast_w1(1, 0, nc.vector.tensor_copy)
+        stage = cast_w1(1, 0, nc.scalar.copy)
         quantize(w1_q[1, 0], whole, stage[:])
         for hf in range(2):
             nc.vector.tensor_copy(v_codes[1][:, half_cols(hf)], table[1][:].indirect(half_list(idx, hf)))
@@ -340,8 +346,8 @@ def tile_list_visit_page_update_kernel(
         x_q = [mx_operand(S, "xq%d" % b) for b in range(PASSES)]
         wn_q = mx_operand(PASSES * N, "wnq")
 
-        def quantize_rows(operand, rows, cols, stage):
-            interleave(rows[:, :, cols], stage)
+        def quantize_rows(operand, rows, cols, stage, negate=False):
+            interleave(rows[:, :, cols], stage, negate)
             quantize(operand, cols, stage[:, 0 : PACK * (cols.stop - cols.start)])
 
         def quantize_wn(a):
@@ -411,12 +417,12 @@ def tile_list_visit_page_update_kernel(
             stage = shared_bf[:, hf * PACK * HALF : (hf + 1) * PACK * HALF]
             quantize_rows(x_q[0], x_rows[0], half_cols(hf), stage)
 
-        quantize_rows(h_q[0], h_t[0], half_cols(0), staging("h_bf00"))
+        quantize_rows(h_q[0], h_t[0], half_cols(0), staging("h_bf00"), True)
         make_h(4, 0)
         scatter_h(4, 0)
         floor_x(2, slice(0, S), picked[0][:])
         gather_x(3, None, picked[1][:])
-        quantize_rows(h_q[0], h_t[0], half_cols(1), staging("h_bf01"))
+        quantize_rows(h_q[0], h_t[0], half_cols(1), staging("h_bf01"), True)
         make_h(5, 0)
         scatter_h(5, 0)
         floor_x(3, slice(0, S), picked[1][:])
@@ -430,13 +436,13 @@ def tile_list_visit_page_update_kernel(
 
         notes = ring.tile([P, OUT_TILES, S], F32, name="notes", tag="big0", bufs=1)
 
-        def natural(bank, nb, cols, weight, data):
+        def natural(bank, nb, cols, weight, data, first=True, last=True):
             for a in reversed(range(PASSES)):
                 w_codes, w_scales = weight(a, nb * P, P)
                 d_codes, d_scales = data(a, cols)
                 nc.tensor.matmul_mx(
                     out=bank, lhsT=w_codes, lhsT_scale=w_scales, rhs=d_codes, rhs_scale=d_scales,
-                    start=(a == PASSES - 1), stop=(a == 0),
+                    start=(first and a == PASSES - 1), stop=(last and a == 0),
                 )
 
         def make_notes(i):
@@ -444,7 +450,11 @@ def tile_list_visit_page_update_kernel(
                 return
             hf, nb = divmod(i, OUT_TILES)
             notes_bank = psum.tile([P, HALF], F32, name="notes_bank", tag="bank_u", bufs=2)
-            natural(notes_bank[:], nb, half_cols(hf), wn_op, v_op)
+            if hf == 0:
+                natural(notes_bank[:], nb, half_cols(hf), wn_op, v_op)
+            else:
+                natural(notes_bank[:], nb, half_cols(hf), wh_op, h_op, last=False)
+                natural(notes_bank[:], nb, half_cols(hf), wn_op, v_op, first=False)
             nc.scalar.copy(notes[:, nb, half_cols(hf)], notes_bank[:])
 
         for s in range(4, 8):
@@ -454,13 +464,13 @@ def tile_list_visit_page_update_kernel(
                 gather_x(s - 1, 0, spent_wgs(s - 1))
                 floor_x(s - 1, whole, spent_wgs(s - 1))
             if s == 4:
-                quantize_rows(h_q[1], h_t[1], half_cols(0), picked[1][:].bitcast(BF16))
+                quantize_rows(h_q[1], h_t[1], half_cols(0), picked[1][:].bitcast(BF16), True)
             if (s, 1) in [(6, 1), (7, 1)]:
                 quantize_x0([(6, 1), (7, 1)].index((s, 1)))
             for jb in ():
                 make_notes(jb)
-        quantize_rows(h_q[1], h_t[1], half_cols(1), staging("h_bf11"))
-        for i in range(2 * OUT_TILES):
+        quantize_rows(h_q[1], h_t[1], half_cols(1), staging("h_bf11"), True)
+        for i in range(OUT_TILES):
             make_notes(i)
         gather_x(6, 0, spent_wgs(6))
         gather_x(7, 0, picked[0][:, whole])
@@ -478,7 +488,18 @@ def tile_list_visit_page_update_kernel(
         gather_x(7, 1, last_picks[3])
         floor_x(6, half_cols(1), last_picks[2])
         floor_x(7, half_cols(1), last_picks[3])
-        quantize_rows(x_q[1], x_rows[1], units[2], staging("x_bf12"))
+        last_stage = staging("x_bf12")
+        quantize_rows(x_q[1], x_rows[1], units[2], last_stage)
+
+        def put_last(nb):
+            unit = half_cols(1)
+            recalled_bank = psum.tile([P, HALF], F32, name="recalled_bank", tag="bank_h", bufs=4)
+            natural(recalled_bank[:], nb, unit, wh_op, h_op, last=False)
+            natural(recalled_bank[:], nb, unit, wr_op, x_op, first=False)
+            y = work("y")[:]
+            nc.vector.tensor_tensor(y, recalled_bank[:], notes[:, nb, unit], ALU.max)
+            nc.vector.tensor_tensor(visit[nb][:].indirect(half_list(late["idx4"], 1)), y, late["wgo"][:, unit], ALU.mult)
+            nc.sync.dma_start(out[nb * P : (nb + 1) * P, :], visit[nb][:])
 
         def put(u, nb):
             unit = units[u]
@@ -490,17 +511,22 @@ def tile_list_visit_page_update_kernel(
             for c0 in range(0, width, step):
                 piece = slice(unit.start + c0, unit.start + c0 + step)
                 natural(recalled_bank[:, c0 : c0 + step], nb, piece, wr_op, x_op)
-            larger = work("larger")[:, 0:width]
+            if u == 1:
+                larger = last_stage[:].bitcast(F32)[:, nb * width : (nb + 1) * width]
+            else:
+                larger = work("larger")[:, 0:width]
             nc.vector.tensor_tensor(larger, recalled_bank[:, 0:width], notes[:, nb, unit], ALU.max)
             y = work("y")[:, 0:width]
-            nc.vector.tensor_tensor(y, larger, state_bank[:, 0:width], ALU.subtract)
+            nc.vector.tensor_tensor(y, larger, state_bank[:, 0:width], ALU.add)
             nc.vector.tensor_tensor(
                 visit[nb][:].indirect(late["idx4"][:, unit.start // 16 : unit.stop // 16]),
                 y, late["wgo"][:, unit], ALU.mult,
             )
 
-        for u in range(len(units)):
+        for u in range(len(units) - 1):
             for nb in range(OUT_TILES):
                 put(u, nb)
-                if u == len(units) - 1:
-                    nc.sync.dma_start(out[nb * P : (nb + 1) * P, :], visit[nb][:])
+                if u == 1:
+                    make_notes(OUT_TILES + nb)
+        for nb in range(OUT_TILES):
+            put_last(nb)

from contextlib import ExitStack

import concourse.mybir as mybir
from concourse.masks import make_identity

K, H, N, T, S, T2 = 1024, 1024, 384, 4096, 1024, 2048
FLOPS = 2 * K * H * S + 3 * 2 * K * N * S

F32 = mybir.dt.float32
BF16 = mybir.dt.bfloat16
I32 = mybir.dt.int32
U32 = mybir.dt.uint32
U16 = mybir.dt.uint16
U8 = mybir.dt.uint8
FP8X4 = mybir.dt.float8_e4m3fn_x4
FP4X4 = mybir.dt.float4_e2m1fn_x4
ALU = mybir.AluOpType
ACT = mybir.ActivationFunctionType

P = 128
PACK = 4
PASS = P * PACK
PASSES = 2
HALF = 512
BLOCKS = HALF // P
OUT_TILES = N // P
LIST_COLS = S // 16
LEAD = 256
DIRECT = []


def tile_list_visit_page_update_kernel(
    tc, tab_words, tab_scales, offs, offs2, offs3, offs4, w1, usual, gain, wgs, page0, low,
    wr_words, wr_scales, wn, wh_words, wh_scales, wgo, page1, out,
):
    nc = tc.nc
    with ExitStack() as ctx:
        lists = ctx.enter_context(tc.tile_pool(name="lists", bufs=1))
        keep = ctx.enter_context(tc.tile_pool(name="keep", bufs=1))
        ring = ctx.enter_context(tc.tile_pool(name="ring", bufs=2))
        psum = ctx.enter_context(tc.psum_pool(name="psum", bufs=2))

        def kept(shape, dtype, name):
            return keep.tile(shape, dtype, name=name, align_bytes=64)

        def half_cols(hf):
            return slice(hf * HALF, (hf + 1) * HALF)

        def half_list(tile, hf):
            return tile[:, hf * LIST_COLS // 2 : (hf + 1) * LIST_COLS // 2]

        def load_list(src, name):
            tile = lists.tile([P, LIST_COLS], U16, name=name)
            nc.sync.dma_start(tile[:], src)
            return tile

        def slice_rows(src, s):
            b, t = divmod(s, PACK)
            return src.rearrange("(b p t) c -> b t p c", b=PASSES, t=PACK)[b, t]

        def load_weight_rows(src, a, cols, name):
            width = cols.stop - cols.start
            raw = ring.tile([P, PACK, width], F32, name=name, tag="raw8k", bufs=3)
            nc.sync.dma_start(raw[:], src[a * PASS : (a + 1) * PASS, cols].rearrange("(p j) c -> p j c", j=PACK))
            return raw

        usual_buf = [kept([P, S], F32, "usual_buf%d" % i) for i in range(4)]

        def load_usual(s):
            nc.sync.dma_start(usual_buf[s % 4][:], slice_rows(usual, s))

        def load_page(s):
            tile = ring.tile([P, T2], F32, name="page%d" % s, tag="page", bufs=5)
            nc.sync.dma_start(tile[:], slice_rows(page0, s))
            return tile

        def load_table(a):
            tile = ring.tile([P, T], U32, name="table%d" % a, tag="big%d" % a, bufs=1)
            nc.sync.dma_start(tile[:].bitcast(I32), tab_words[a].rearrange("p n t -> p (n t)").bitcast(I32))
            return tile

        def load_weight_scales(src, name):
            tile = kept([P, PASSES, N], U8, name)
            nc.vector.memset(tile[:].rearrange("p a n -> p (a n)").bitcast(I32), 0)
            return tile

        def fill_weight_scales(tile, src):
            for q in range(4):
                nc.sync.dma_start(
                    tile[32 * q : 32 * q + 4, :, :].bitcast(I32),
                    src[:, 4 * q : 4 * q + 4, :].rearrange("a r n -> r a n").bitcast(I32),
                )

        table_scales = ring.tile([P, T], U8, name="table_scales", tag="early_late", bufs=1)
        nc.vector.memset(table_scales[:].bitcast(I32), 0)
        warm = kept([P, 8], F32, "warm")
        nc.vector.memset(warm[:], 1.0)
        nc.scalar.activation(warm[:], warm[:], ACT.Ln)
        wr_sc = load_weight_scales(wr_scales, "wr_sc")
        wh_sc = load_weight_scales(wh_scales, "wh_sc")
        ident = kept([P, P], F32, "ident")
        make_identity(nc, ident[:])

        w1_raw = {}
        idx = load_list(offs, "idx")
        scale_rows = ring.tile([P, T], U8, name="scale_rows", tag="staging", bufs=3, align_bytes=64)
        for q in range(4):
            nc.sync.dma_start(
                scale_rows[32 * q : 32 * q + 4, :].bitcast(I32),
                tab_scales[0, 4 * q : 4 * q + 4, :].bitcast(I32),
            )
        w1_raw[0, 0] = load_weight_rows(w1, 0, half_cols(0), "w1_raw00")
        table = [load_table(0)]
        w1_raw[1, 0] = load_weight_rows(w1, 1, half_cols(0), "w1_raw10")
        for q in range(4):
            nc.sync.dma_start(
                table_scales[32 * q + 4 : 32 * q + 8, :].bitcast(I32),
                tab_scales[1, 4 * q : 4 * q + 4, :].bitcast(I32),
            )
        table.append(load_table(1))
        gain_t = kept([P, PASSES, PACK], F32, "gain_t")
        nc.sync.dma_start(gain_t[:], gain.rearrange("(b p t) -> p b t", b=PASSES, t=PACK))
        idx2 = load_list(offs2, "idx2")
        lead = slice(0, LEAD)
        rest = slice(LEAD, S)
        nc.sync.dma_start(usual_buf[0][:, lead], slice_rows(usual, 0)[:, lead])
        page = [load_page(0)]
        wgs_rows = wgs.rearrange("(i t) j -> i t j", t=PACK)
        wgs_t = [kept([P, S], F32, "wgs%d" % t) for t in range(PACK)]

        def load_wgs(t, cols=slice(0, S)):
            for q in (0, 2, 1, 3):
                nc.sync.dma_start(wgs_t[t][32 * q : 32 * q + 32, cols], wgs_rows[:, t, cols])

        load_wgs(0, lead)
        nc.sync.dma_start(usual_buf[0][:, rest], slice_rows(usual, 0)[:, rest])
        load_wgs(0, rest)
        load_usual(1)
        idx3 = load_list(offs3, "idx3")
        low_t = kept([P, PASSES, PACK], F32, "low_t")
        nc.sync.dma_start(low_t[:], low.rearrange("(b p t) -> p b t", b=PASSES, t=PACK))
        load_wgs(1)
        page.append(load_page(1))
        load_usual(2)
        w1_raw[0, 1] = load_weight_rows(w1, 0, half_cols(1), "w1_raw01")
        w1_raw[1, 1] = load_weight_rows(w1, 1, half_cols(1), "w1_raw11")
        load_usual(3)
        load_wgs(2)
        page.append(load_page(2))
        load_wgs(3)
        page.append(load_page(3))
        wn_raw = [load_weight_rows(wn, a, slice(0, N), "wn_raw%d" % a) for a in range(PASSES)]
        wr_t = kept([P, PASSES, 2 * N], U8, "wr_t")
        wh_t = kept([P, PASSES, N], U32, "wh_t")
        late = {}
        visit = []

        def last_loads():
            fill_weight_scales(wr_sc, wr_scales)
            fill_weight_scales(wh_sc, wh_scales)
            nc.sync.dma_start(wr_t[:].bitcast(I32), wr_words.rearrange("a p c -> p a c").bitcast(I32))
            nc.sync.dma_start(wh_t[:].bitcast(I32), wh_words.rearrange("a p n t -> p a (n t)").bitcast(I32))
            late["idx4"] = load_list(offs4, "idx4")
            late["wgo"] = ring.tile([P, S], F32, name="wgo_t", tag="early_late", bufs=1)
            nc.sync.dma_start(late["wgo"][:], wgo)
            for nb in range(OUT_TILES):
                tile = ring.tile([P, T2], F32, name="visit%d" % nb, tag="raw8k", bufs=3)
                nc.sync.dma_start(tile[:], page1[nb * P : (nb + 1) * P, :])
                visit.append(tile)

        def wgs_slice(t):
            return wgs_t[t][:]

        def staging(name):
            return ring.tile([P, PACK * HALF], BF16, name=name, tag="staging", bufs=3, align_bytes=64)

        def mx_operand(width, name):
            return kept([P, width], U32, name + "_codes"), kept([P, width], U8, name + "_scales")

        def quantize(operand, cols, src):
            codes, scales = operand
            nc.vector.quantize_mx(out=codes[:, cols].bitcast(FP8X4), scales=scales[:, cols], in_=src)

        def cast_w1(a, b, copy):
            stage = staging("w1_bf%d%d" % (a, b))
            copy(
                stage[:].rearrange("p (t m j) -> p m t j", t=PACK, j=PACK),
                w1_raw[a, b][:].rearrange("p j (m t) -> p m t j", t=PACK),
            )
            return stage

        def interleave(src, stage, negate=False):
            width = src.shape[2]
            dst = stage[:, 0 : PACK * width].rearrange("p (c t) -> p c t", t=PACK)
            if negate:
                nc.scalar.activation(dst, src.rearrange("p t c -> p c t"), ACT.Copy, scale=-1.0)
            else:
                nc.scalar.copy(dst, src.rearrange("p t c -> p c t"))
            return stage

        def work(name):
            return ring.tile([P, HALF], F32, name=name, tag="work", bufs=5)

        def add_transposed(dst, first, second):
            nc.tensor.matmul(dst, lhsT=first, rhs=ident[:], is_transpose=True, start=True, stop=False)
            nc.tensor.matmul(dst, lhsT=second, rhs=ident[:], is_transpose=True, start=False, stop=True)

        w1_q = {}
        for a in range(PASSES):
            for b in range(PASSES):
                w1_q[a, b] = mx_operand(HALF, "w1q%d%d" % (a, b))
        v_scales = kept([P, S], U8, "v_scales")
        v_codes = [kept([P, S], U32, "v_codes%d" % a) for a in range(PASSES)]
        whole = slice(0, HALF)
        stage = cast_w1(0, 0, nc.vector.tensor_copy)
        for q in range(4):
            rows = slice(32 * q, 32 * q + 4)
            nc.vector.tensor_copy(table_scales[rows, :].bitcast(I32), scale_rows[rows, :].bitcast(I32))
        nc.vector.tensor_copy(v_scales[:], table_scales[:].indirect(idx[:]))
        quantize(w1_q[0, 0], whole, stage[:])
        nc.vector.tensor_copy(v_codes[0][:], table[0][:].indirect(idx[:]))
        stage = cast_w1(1, 0, nc.scalar.copy)
        quantize(w1_q[1, 0], whole, stage[:])
        for hf in range(2):
            nc.vector.tensor_copy(v_codes[1][:, half_cols(hf)], table[1][:].indirect(half_list(idx, hf)))

        h_t = {}
        picked = [kept([P, S], F32, "picked%d" % i) for i in range(2)]
        shared = kept([P, 2 * S], F32, "shared")

        def make_direct_h(s, hf):
            b, t = divmod(s, PACK)
            cols = half_cols(hf)
            gain_col = gain_t[:, b, t : t + 1]
            scaled = usual_buf[s % 4][:, cols]
            nc.scalar.activation(scaled, scaled, ACT.Copy, scale=gain_col)
            a_bank = psum.tile([P, HALF], F32, name="a_direct", tag="bank_a", bufs=2)
            for a in range(PASSES):
                codes, scales = w1_q[a, b]
                nc.tensor.matmul_mx(
                    out=a_bank[:],
                    lhsT=codes[:, t * P : (t + 1) * P].bitcast(FP8X4),
                    lhsT_scale=scales[:, t * P : (t + 1) * P],
                    rhs=v_codes[a][:, cols].bitcast(FP8X4),
                    rhs_scale=v_scales[4 * a : P, cols],
                    start=(a == 0),
                    stop=(a == PASSES - 1),
                )
            if (s, hf) in [(6, 1), (7, 1)]:
                logs = shared[:, [(6, 1), (7, 1)].index((s, hf)) * S :][:, whole]
            else:
                logs = work("logs")[:]
            nc.scalar.activation(logs, a_bank[:], ACT.Abs)
            nc.scalar.activation(logs, logs, ACT.Ln, bias=1.0)
            nc.vector.scalar_tensor_tensor(h_t[b][:, t, cols], logs, gain_col, scaled, ALU.mult, ALU.subtract)

        def make_h(s, hf):
            b, t = divmod(s, PACK)
            if b not in h_t:
                h_t[b] = ring.tile([P, PACK, S], F32, name="h%d" % b, tag="big%d" % b, bufs=1)
            if (s, hf) in DIRECT:
                make_direct_h(s, hf)
                return
            usual_bank = psum.tile([P, HALF], F32, name="usual_bank", tag="bank_u", bufs=2)
            for jb in range(BLOCKS):
                j0 = hf * HALF + jb * P
                nc.tensor.transpose(usual_bank[:, jb * P : (jb + 1) * P], usual_buf[s % 4][:, j0 : j0 + P], ident[:])
            neg_usual = work("neg_usual")
            nc.scalar.activation(neg_usual[:], usual_bank[:], ACT.Copy, scale=-1.0)
            a_bank = psum.tile([P, HALF], F32, name="a_bank", tag="bank_a", bufs=2)
            for jb in range(BLOCKS):
                j0 = hf * HALF + jb * P
                for a in range(PASSES):
                    codes, scales = w1_q[a, b]
                    nc.tensor.matmul_mx(
                        out=a_bank[:, jb * P : (jb + 1) * P],
                        lhsT=v_codes[a][:, j0 : j0 + P].bitcast(FP8X4),
                        lhsT_scale=v_scales[4 * a : P, j0 : j0 + P],
                        rhs=codes[:, t * P : (t + 1) * P].bitcast(FP8X4),
                        rhs_scale=scales[:, t * P : (t + 1) * P],
                        start=(a == 0),
                        stop=(a == PASSES - 1),
                    )
            if (s, hf) in [(6, 1), (7, 1)]:
                logs = shared[:, [(6, 1), (7, 1)].index((s, hf)) * S :][:, whole]
            elif (s, hf) == (4, 1):
                logs = picked[1][:, whole]
            else:
                logs = work("logs")[:]
            nc.scalar.activation(logs, a_bank[:], ACT.Abs)
            nc.scalar.activation(logs, logs, ACT.Ln, bias=1.0)
            h_bank = psum.tile([P, HALF], F32, name="h_bank", tag="bank_h", bufs=4)
            for jb in range(BLOCKS):
                cols = slice(jb * P, (jb + 1) * P)
                add_transposed(h_bank[:, cols], neg_usual[:, cols], logs[:, cols])
            nc.scalar.activation(h_t[b][:, t, half_cols(hf)], h_bank[:], ACT.Copy, scale=gain_t[:, b, t : t + 1])

        def make_first_h(cols):
            width = cols.stop - cols.start
            a_bank = psum.tile([P, HALF], F32, name="a_first", tag="bank_a", bufs=2)
            for a in range(PASSES):
                codes, scales = w1_q[a, 0]
                nc.tensor.matmul_mx(
                    out=a_bank[:, 0:width],
                    lhsT=codes[:, 0:P].bitcast(FP8X4),
                    lhsT_scale=scales[:, 0:P],
                    rhs=v_codes[a][:, cols].bitcast(FP8X4),
                    rhs_scale=v_scales[4 * a : P, cols],
                    start=(a == 0),
                    stop=(a == PASSES - 1),
                )
            logs = work("logs_first")[:, 0:width]
            nc.scalar.activation(logs, a_bank[:, 0:width], ACT.Abs)
            nc.scalar.activation(logs, logs, ACT.Ln, bias=1.0)
            diff = work("diff_first")[:, 0:width]
            nc.vector.tensor_tensor(diff, logs, usual_buf[0][:, cols], ALU.subtract)
            nc.vector.tensor_scalar(h_t[0][:, 0, cols], diff, gain_t[:, 0, 0:1], None, op0=ALU.mult)
            nc.vector.tensor_tensor(
                page[0][:].indirect(idx2[:, cols.start // 16 : cols.stop // 16]), h_t[0][:, 0, cols],
                wgs_t[0][:, cols], ALU.mult,
            )

        def scatter_h(s, hf):
            b, t = divmod(s, PACK)
            if hf is None:
                nc.vector.tensor_tensor(page[s][:].indirect(idx2[:]), h_t[b][:, t, :], wgs_slice(t), ALU.mult)
            else:
                nc.vector.tensor_tensor(
                    page[s][:].indirect(half_list(idx2, hf)), h_t[b][:, t, half_cols(hf)],
                    wgs_slice(t)[:, half_cols(hf)], ALU.mult,
                )

        x_rows = [kept([P, PACK, S], BF16, "x_rows%d" % b) for b in range(PASSES)]

        def gather_x(s, hf, dst):
            if hf is None:
                nc.vector.tensor_copy(dst, page[s][:].indirect(idx3[:]))
            else:
                nc.vector.tensor_copy(dst, page[s][:].indirect(half_list(idx3, hf)))

        def floor_x(s, cols, src):
            b, t = divmod(s, PACK)
            nc.vector.tensor_scalar(x_rows[b][:, t, cols], src, low_t[:, b, t : t + 1], None, op0=ALU.max)

        h_q = [mx_operand(S, "hq%d" % b) for b in range(PASSES)]
        x_q = [mx_operand(S, "xq%d" % b) for b in range(PASSES)]
        wn_q = mx_operand(PASSES * N, "wnq")

        def quantize_rows(operand, rows, cols, stage, negate=False):
            interleave(rows[:, :, cols], stage, negate)
            quantize(operand, cols, stage[:, 0 : PACK * (cols.stop - cols.start)])

        def quantize_wn(a):
            stage = interleave(wn_raw[a][:], shared[:, a * S : (a + 1) * S].bitcast(BF16))
            quantize(wn_q, slice(a * N, a * N + 256), stage[:, 0:1024])
            quantize(wn_q, slice(a * N + 256, (a + 1) * N), stage[:, 1024 : PACK * N])

        units = [slice(0, 256), slice(256, 512), slice(512, 1024)]

        def products(bank, j0, lhs, rhs, widths):
            n0 = 0
            for width in widths:
                for a in reversed(range(PASSES)):
                    l_codes, l_scales = lhs(a, slice(j0, j0 + P))
                    r_codes, r_scales = rhs(a, n0, width)
                    nc.tensor.matmul_mx(
                        out=bank[:, n0 : n0 + width], lhsT=l_codes, lhsT_scale=l_scales,
                        rhs=r_codes, rhs_scale=r_scales, start=(a == PASSES - 1), stop=(a == 0),
                    )
                n0 = n0 + width

        def v_op(a, cols):
            return v_codes[a][:, cols].bitcast(FP8X4), v_scales[4 * a : P, cols]

        def h_op(a, cols):
            return h_q[a][0][:, cols].bitcast(FP8X4), h_q[a][1][:, cols]

        def x_op(a, cols):
            return x_q[a][0][:, cols].bitcast(FP8X4), x_q[a][1][:, cols]

        def wn_op(a, n0, width):
            cols = slice(a * N + n0, a * N + n0 + width)
            return wn_q[0][:, cols].bitcast(FP8X4), wn_q[1][:, cols]

        def wh_op(a, n0, width):
            return wh_t[:, a, n0 : n0 + width].bitcast(FP8X4), wh_sc[:, a, n0 : n0 + width]

        def wr_op(a, n0, width):
            return wr_t[:, a, 2 * n0 : 2 * (n0 + width)].bitcast(FP4X4), wr_sc[:, a, n0 : n0 + width]

        h_t[0] = ring.tile([P, PACK, S], F32, name="h0", tag="big0", bufs=1)
        for cols in (slice(0, 256), slice(256, 512), slice(512, 1024)):
            make_first_h(cols)
        load_usual(4)
        page.append(load_page(4))
        for hf in range(2):
            make_h(1, hf)
        load_usual(5)
        scatter_h(1, None)
        gather_x(0, None, picked[0][:])
        for s in (2, 3):
            for hf in range(2):
                make_h(s, hf)
            load_usual(s + 4)
            if s == 2:
                for a in range(PASSES):
                    quantize(w1_q[a, 1], whole, cast_w1(a, 1, nc.scalar.copy)[:])
            scatter_h(s, None)
            floor_x(s - 2, slice(0, S), picked[s % 2][:])
            gather_x(s - 1, None, picked[(s - 1) % 2][:])
        for s in range(5, 8):
            page.append(load_page(s))
        last_loads()
        shared_bf = shared[:].bitcast(BF16)

        def quantize_x0(hf):
            stage = shared_bf[:, hf * PACK * HALF : (hf + 1) * PACK * HALF]
            quantize_rows(x_q[0], x_rows[0], half_cols(hf), stage)

        quantize_rows(h_q[0], h_t[0], half_cols(0), staging("h_bf00"), True)
        make_h(4, 0)
        scatter_h(4, 0)
        floor_x(2, slice(0, S), picked[0][:])
        gather_x(3, None, picked[1][:])
        quantize_rows(h_q[0], h_t[0], half_cols(1), staging("h_bf01"), True)
        make_h(5, 0)
        scatter_h(5, 0)
        floor_x(3, slice(0, S), picked[1][:])
        for s in (6, 7):
            quantize_wn(s - 6)
            make_h(s, 0)
            scatter_h(s, 0)

        def spent_wgs(s):
            return wgs_slice(s + 1 - PACK)[:, half_cols(1)]

        notes = ring.tile([P, OUT_TILES, S], F32, name="notes", tag="big0", bufs=1)

        def natural(bank, nb, cols, weight, data, first=True, last=True):
            for a in reversed(range(PASSES)):
                w_codes, w_scales = weight(a, nb * P, P)
                d_codes, d_scales = data(a, cols)
                nc.tensor.matmul_mx(
                    out=bank, lhsT=w_codes, lhsT_scale=w_scales, rhs=d_codes, rhs_scale=d_scales,
                    start=(first and a == PASSES - 1), stop=(last and a == 0),
                )

        def make_notes(i):
            if i >= 2 * OUT_TILES:
                return
            hf, nb = divmod(i, OUT_TILES)
            notes_bank = psum.tile([P, HALF], F32, name="notes_bank", tag="bank_u", bufs=2)
            if hf == 0:
                natural(notes_bank[:], nb, half_cols(hf), wn_op, v_op)
            else:
                natural(notes_bank[:], nb, half_cols(hf), wh_op, h_op, last=False)
                natural(notes_bank[:], nb, half_cols(hf), wn_op, v_op, first=False)
            nc.scalar.copy(notes[:, nb, half_cols(hf)], notes_bank[:])

        for s in range(4, 8):
            make_h(s, 1)
            scatter_h(s, 1)
            if s in (5, 6):
                gather_x(s - 1, 0, spent_wgs(s - 1))
                floor_x(s - 1, whole, spent_wgs(s - 1))
            if s == 4:
                quantize_rows(h_q[1], h_t[1], half_cols(0), picked[1][:].bitcast(BF16), True)
            if (s, 1) in [(6, 1), (7, 1)]:
                quantize_x0([(6, 1), (7, 1)].index((s, 1)))
            for jb in ():
                make_notes(jb)
        quantize_rows(h_q[1], h_t[1], half_cols(1), staging("h_bf11"), True)
        for i in range(OUT_TILES):
            make_notes(i)
        gather_x(6, 0, spent_wgs(6))
        gather_x(7, 0, picked[0][:, whole])
        floor_x(6, whole, spent_wgs(6))
        floor_x(7, whole, picked[0][:, whole])
        x_stage = [staging("x_bf1%d" % u) for u in range(2)]
        for u in range(2):
            quantize_rows(x_q[1], x_rows[1], units[u], x_stage[u])
        last_picks = [spent_wgs(6), picked[0][:, whole]] + [x_stage[u][:].bitcast(F32)[:, whole] for u in range(2)]
        gather_x(4, 1, last_picks[0])
        gather_x(5, 1, last_picks[1])
        floor_x(4, half_cols(1), last_picks[0])
        gather_x(6, 1, last_picks[2])
        floor_x(5, half_cols(1), last_picks[1])
        gather_x(7, 1, last_picks[3])
        floor_x(6, half_cols(1), last_picks[2])
        floor_x(7, half_cols(1), last_picks[3])
        last_stage = staging("x_bf12")
        quantize_rows(x_q[1], x_rows[1], units[2], last_stage)

        def put_last(nb):
            unit = half_cols(1)
            recalled_bank = psum.tile([P, HALF], F32, name="recalled_bank", tag="bank_h", bufs=4)
            natural(recalled_bank[:], nb, unit, wh_op, h_op, last=False)
            natural(recalled_bank[:], nb, unit, wr_op, x_op, first=False)
            y = work("y")[:]
            nc.vector.tensor_tensor(y, recalled_bank[:], notes[:, nb, unit], ALU.max)
            nc.vector.tensor_tensor(visit[nb][:].indirect(half_list(late["idx4"], 1)), y, late["wgo"][:, unit], ALU.mult)
            nc.sync.dma_start(out[nb * P : (nb + 1) * P, :], visit[nb][:])

        def put(u, nb):
            unit = units[u]
            width = unit.stop - unit.start
            state_bank = psum.tile([P, HALF], F32, name="state_bank", tag="bank_h", bufs=4)
            natural(state_bank[:, 0:width], nb, unit, wh_op, h_op)
            recalled_bank = psum.tile([P, HALF], F32, name="recalled_bank", tag="bank_a", bufs=2)
            step = HALF if width == HALF else P
            for c0 in range(0, width, step):
                piece = slice(unit.start + c0, unit.start + c0 + step)
                natural(recalled_bank[:, c0 : c0 + step], nb, piece, wr_op, x_op)
            if u == 1:
                larger = last_stage[:].bitcast(F32)[:, nb * width : (nb + 1) * width]
            else:
                larger = work("larger")[:, 0:width]
            nc.vector.tensor_tensor(larger, recalled_bank[:, 0:width], notes[:, nb, unit], ALU.max)
            y = work("y")[:, 0:width]
            nc.vector.tensor_tensor(y, larger, state_bank[:, 0:width], ALU.add)
            nc.vector.tensor_tensor(
                visit[nb][:].indirect(late["idx4"][:, unit.start // 16 : unit.stop // 16]),
                y, late["wgo"][:, unit], ALU.mult,
            )

        for u in range(len(units) - 1):
            for nb in range(OUT_TILES):
                put(u, nb)
                if u == 1:
                    make_notes(OUT_TILES + nb)
        for nb in range(OUT_TILES):
            put_last(nb)
